import numpy as np
import ml_dtypes


def mxq(x, axis, fmt="e4m3"):
    dtype, down = {"e4m3": (ml_dtypes.float8_e4m3fn, 7), "e5m2": (ml_dtypes.float8_e5m2, 14)}[fmt]
    v = np.moveaxis(np.asarray(x, np.float32).astype(ml_dtypes.bfloat16).astype(np.float64), axis, -1)
    blocks = v.reshape(v.shape[:-1] + (-1, 32))
    amax = np.abs(blocks).max(-1, keepdims=True)
    byte = np.maximum(np.where(amax > 0, np.frexp(amax)[1] - 1 + 127, 0) - down, 1)
    scale = np.exp2(byte - 127.0)
    codes = (blocks / scale).astype(np.float32).astype(dtype).astype(np.float64)
    return np.moveaxis((codes * scale).reshape(v.shape), -1, axis)


WIDE = False


def mx_kscale(k):
    if not WIDE:
        return np.ones(k)
    levels = np.array([10, -10, 5, -5, 0])
    if k % 512:
        return np.exp2(np.random.permutation(np.resize(levels, k // 32))).repeat(32)
    a = np.empty((k // 512, 16))
    for p in range(k // 512):
        a[p, :8] = np.random.permutation(np.resize(levels, 8))
        for g in range(8):
            far = levels[np.abs(levels - a[p, g]) >= 10]
            a[p, g + 8] = far[np.random.randint(len(far))]
    return np.exp2(a.ravel()).repeat(32)


def f64(x):
    return np.asarray(x).astype(np.float64)


def striped(idx):
    return np.tile(idx.reshape(-1, 16).T, (8, 1)).astype(np.uint16)


def unstriped(offs):
    return offs[:16].T.reshape(-1).astype(np.int64)


E2M1 = np.array([0.0, 0.5, 1.0, 1.5, 2.0, 3.0, 4.0, 6.0, -0.0, -0.5, -1.0, -1.5, -2.0, -3.0, -4.0, -6.0])


def pack_weight(w, fmt):
    k, n = w.shape
    w = f64(np.asarray(w, np.float32).astype(ml_dtypes.bfloat16)).reshape(k // 32, 32, n)
    amax = np.abs(w).max(1)
    if fmt == "e4m3":
        byte = np.frexp(amax)[1] - 1 + 127 - 7
    else:
        mant, ex = np.frexp(amax / 6.0)
        byte = np.where(mant > 0.5, ex, ex - 1) + 127
    byte = np.clip(np.where(amax > 0, byte, 1), 1, 254)
    scaled = (w * np.exp2(127.0 - byte)[:, None, :]).reshape(k, n).astype(np.float32)
    by_word = np.ascontiguousarray(scaled.reshape(k // 512, 128, 4, n).transpose(0, 1, 3, 2))
    if fmt == "e4m3":
        words = by_word.astype(ml_dtypes.float8_e4m3fn).view(np.uint8)
    else:
        c = by_word.astype(ml_dtypes.float4_e2m1fn).view(np.uint8) & 0xF
        words = (c[..., 0::2] | (c[..., 1::2] << 4)).reshape(k // 512, 128, 2 * n)
    return np.ascontiguousarray(words), np.ascontiguousarray(byte.astype(np.uint8).reshape(k // 512, 16, n))


def unpack_weight(words, scales, fmt):
    g, _, n = scales.shape
    words = np.ascontiguousarray(words).reshape(g, 128, n, -1)
    if fmt == "e4m3":
        vals = words.view(ml_dtypes.float8_e4m3fn).astype(np.float64)
    else:
        nib = np.empty((g, 128, n, 4), np.uint8)
        nib[..., 0::2] = words & 0xF
        nib[..., 1::2] = words >> 4
        vals = E2M1[nib]
    vals = vals * np.repeat(np.exp2(scales.astype(np.float64) - 127.0), 8, axis=1)[..., None]
    return vals.transpose(0, 1, 3, 2).reshape(g * 512, n)


K, T, E, C, N = 2560, 1536, 8, 128, 128


def by_expert(wq, xq):
    return np.concatenate([wq[e].T @ xq[:, e * C:(e + 1) * C] for e in range(E)], axis=1)


def setup_inputs():
    n = np.random.standard_normal
    s = mx_kscale(K)[:, None]
    x = pack_weight(n((K, T)) * s, "e4m3")
    return {
        "x_words": x[0],
        "x_scales": x[1],
        "w": (n((E, K, N)) / np.sqrt(K) / s[None]).astype(np.float32),
        "b": (0.3 * n((N, E))).astype(np.float32),
        "gate": np.tile(np.random.uniform(0.2, 1.0, E * C), (N, 1)).astype(np.float32),
        "offs": striped(np.random.permutation(T)[:E * C]),
        "dst": striped(np.random.permutation(T)[:E * C]),
    }


def reference(x_words, x_scales, w, b, gate, offs, dst):
    idx = unstriped(offs)
    xq = unpack_weight(x_words, x_scales, "e4m3")[:, idx]
    y = by_expert(mxq(f64(w), 1, "e4m3"), xq)
    y = y + np.repeat(f64(b), C, axis=1)
    out = np.zeros((N, T))
    out[:, unstriped(dst)] = f64(gate) * y
    return out

@@ -1,0 +1,183 @@
+from contextlib import ExitStack
+
+import concourse.mybir as mybir
+
+K, T, E, C, N = 2560, 1536, 8, 128, 128
+SLOTS = E * C
+FLOPS = 2 * K * N * SLOTS
+
+F32 = mybir.dt.float32
+BF16 = mybir.dt.bfloat16
+I32 = mybir.dt.int32
+U32 = mybir.dt.uint32
+U16 = mybir.dt.uint16
+U8 = mybir.dt.uint8
+FP8X4 = mybir.dt.float8_e4m3fn_x4
+ADD = mybir.AluOpType.add
+MULT = mybir.AluOpType.mult
+
+P = 128
+PACK = 4
+PASSES = K // (P * PACK)
+UNITS = E * PASSES
+CHUNKS = [2] * 19 + [1, 1]
+ON_VECTOR = ()
+SCATTER_CUTS = (0, 256, 512, 832, 1024)
+LAST_SPLIT = 48
+
+
+def tile_moe_two_lin_bias_kernel(tc, x_words, x_scales, w, b, gate, offs, dst, out):
+    nc = tc.nc
+    with ExitStack() as ctx:
+        keep = ctx.enter_context(tc.tile_pool(name="keep", bufs=1))
+        psum = ctx.enter_context(tc.psum_pool(name="psum", bufs=1))
+
+        offs_sb = keep.tile([P, SLOTS // 16], U16, name="offs_sb")
+        dst_sb = keep.tile([P, SLOTS // 16], U16, name="dst_sb")
+        b_sb = keep.tile([P, E], F32, name="b_sb")
+        gate_sb = keep.tile([P, SLOTS], F32, name="gate_sb")
+        y_sb = keep.tile([P, SLOTS], F32, name="y_sb")
+        out_sb = keep.tile([P, T], F32, name="out_sb")
+        tok_words = [keep.tile([P, T], I32, name="tok_words%d" % a, align_bytes=64) for a in range(PASSES)]
+        slot_words = [keep.tile([P, SLOTS], U32, name="slot_words%d" % a, align_bytes=64) for a in range(PASSES)]
+        tok_scales = keep.tile([P, T], U8, name="tok_scales", align_bytes=64)
+        tok_scales_last = keep.tile([P, T], U8, name="tok_scales_last", align_bytes=64)
+        slot_scales = keep.tile([P, SLOTS], U8, name="slot_scales", align_bytes=64)
+        slot_scales_last = keep.tile([P, SLOTS], U8, name="slot_scales_last", align_bytes=64)
+        acc = [psum.tile([P, C], F32, name="acc%d" % e) for e in range(E)]
+
+        first_unit = [sum(CHUNKS[:c]) for c in range(len(CHUNKS))]
+        w_raw = [keep.tile([P, u, PACK, N], F32, name="w_raw%d" % c) for c, u in enumerate(CHUNKS)]
+        w_bf = [keep.tile([P, u, N, PACK], BF16, name="w_bf%d" % c, align_bytes=64) for c, u in enumerate(CHUNKS)]
+        w_codes = [keep.tile([P, u, N], U32, name="w_codes%d" % c, align_bytes=64) for c, u in enumerate(CHUNKS)]
+        w_scales = [keep.tile([P, u, N], U8, name="w_scales%d" % c, align_bytes=64) for c, u in enumerate(CHUNKS)]
+        w_rows = w.rearrange("e k n -> (e k) n")
+
+        nc.gpsimd.memset(tok_scales[:].bitcast(I32), 0)
+        nc.gpsimd.memset(tok_scales_last[:].bitcast(I32), 0)
+        nc.gpsimd.memset(out_sb[:], 0.0)
+
+        def load_scales(q):
+            nc.sync.dma_start(
+                out=tok_scales[32 * q : 32 * q + 16, :].bitcast(I32),
+                in_=x_scales[0:4, 4 * q : 4 * q + 4, :].bitcast(I32),
+            )
+
+        def load_scales_last(q):
+            nc.sync.dma_start(
+                out=tok_scales_last[32 * q : 32 * q + 4, :].bitcast(I32),
+                in_=x_scales[4, 4 * q : 4 * q + 4, :].bitcast(I32),
+            )
+
+        def load_tokens(a):
+            nc.sync.dma_start(out=tok_words[a][:], in_=x_words[a].rearrange("p t r -> p (t r)").bitcast(I32))
+
+        def load_w(c):
+            rows = w_rows[first_unit[c] * P * PACK : (first_unit[c] + CHUNKS[c]) * P * PACK, :]
+            nc.sync.dma_start(
+                out=w_raw[c][:].rearrange("p u j n -> p u (j n)"),
+                in_=rows.rearrange("(u p j) n -> p u (j n)", p=P, j=PACK),
+            )
+
+        nc.sync.dma_start(offs_sb[:], offs)
+        load_tokens(0)
+        load_w(0)
+        for q in range(4):
+            load_scales(q)
+        load_tokens(1)
+        load_w(1)
+        load_tokens(2)
+        load_w(2)
+        for q in range(4):
+            load_scales_last(q)
+        load_tokens(3)
+        load_w(3)
+        load_tokens(4)
+        load_w(4)
+        nc.sync.dma_start(dst_sb[:], dst)
+        nc.sync.dma_start(out=b_sb[:], in_=b)
+        nc.sync.dma_start(out=gate_sb[:], in_=gate)
+        for c in range(PASSES, len(CHUNKS)):
+            load_w(c)
+
+        def gather_words(a):
+            nc.vector.tensor_copy(slot_words[a][:], tok_words[a][:].bitcast(U32).indirect(offs_sb[:]))
+
+        def round_cols(engine, c, i, n0, n1):
+            src = w_raw[c][:, i, :, n0:n1].rearrange("p j (g m) -> p g j m", m=4)
+            tgt = w_bf[c][:, i, n0:n1, :].rearrange("p (g m) j -> p g j m", m=4)
+            if engine == "vector":
+                nc.vector.tensor_copy(out=tgt, in_=src)
+            else:
+                nc.scalar.copy(out=tgt, in_=src)
+
+        def round_chunk(c):
+            for i in range(CHUNKS[c]):
+                unit = first_unit[c] + i
+                if unit == UNITS - 1:
+                    round_cols("scalar", c, i, 0, LAST_SPLIT)
+                    round_cols("vector", c, i, LAST_SPLIT, N)
+                else:
+                    round_cols("vector" if unit in ON_VECTOR else "scalar", c, i, 0, N)
+
+        def quantize_chunk(c):
+            nc.vector.quantize_mx(
+                out=w_codes[c][:].rearrange("p u n -> p (u n)").bitcast(FP8X4),
+                scales=w_scales[c][:].rearrange("p u n -> p (u n)"),
+                in_=w_bf[c][:].rearrange("p u n j -> p (u n j)"),
+            )
+
+        def multiply(unit):
+            e, a = divmod(unit, PASSES)
+            c = max(cc for cc in range(len(CHUNKS)) if first_unit[cc] <= unit)
+            i = unit - first_unit[c]
+            cols = slice(e * C, (e + 1) * C)
+            rhs_scale = slot_scales[4 * a :, cols] if a < 4 else slot_scales_last[:, cols]
+            nc.tensor.matmul_mx(
+                out=acc[e][:],
+                lhsT=w_codes[c][:, i, :].bitcast(FP8X4),
+                lhsT_scale=w_scales[c][:, i, :],
+                rhs=slot_words[a][:, cols].bitcast(FP8X4),
+                rhs_scale=rhs_scale,
+                start=(a == 0),
+                stop=(a == PASSES - 1),
+            )
+
+        def finish_expert(e):
+            cols = slice(e * C, (e + 1) * C)
+            nc.vector.scalar_tensor_tensor(
+                out=y_sb[:, cols], in0=acc[e][:], scalar=b_sb[:, e : e + 1], in1=gate_sb[:, cols], op0=ADD, op1=MULT
+            )
+
+        def scatter(s0, s1):
+            nc.vector.tensor_copy(out_sb[:].indirect(dst_sb[:, s0 // 16 : s1 // 16]), y_sb[:, s0:s1])
+
+        gather_words(0)
+        nc.vector.tensor_copy(slot_scales[:], tok_scales[:].indirect(offs_sb[:]))
+        for a in range(1, PASSES):
+            round_chunk(a - 1)
+            gather_words(a)
+            if a == 2:
+                nc.vector.tensor_copy(slot_scales_last[:], tok_scales_last[:].indirect(offs_sb[:]))
+            quantize_chunk(a - 1)
+
+        done_units = 0
+        done_experts = 0
+        done_cuts = 0
+        for c in range(PASSES - 1, len(CHUNKS) + 1):
+            if c < len(CHUNKS):
+                round_chunk(c)
+            ready_units = first_unit[c] if c < len(CHUNKS) else UNITS
+            for unit in range(done_units, ready_units):
+                multiply(unit)
+            done_units = ready_units
+            if c < len(CHUNKS):
+                quantize_chunk(c)
+            for e in range(done_experts, done_units // PASSES):
+                finish_expert(e)
+            done_experts = done_units // PASSES
+            while done_cuts + 1 < len(SCATTER_CUTS) and SCATTER_CUTS[done_cuts + 1] <= done_experts * C:
+                scatter(SCATTER_CUTS[done_cuts], SCATTER_CUTS[done_cuts + 1])
+                done_cuts += 1
+
+        nc.sync.dma_start(out=out, in_=out_sb[:])

@@ -21,52 +21,55 @@ PACK = 4
 PASSES = K // (P * PACK)
 UNITS = E * PASSES
 CHUNKS = [2] * 19 + [1, 1]
-ON_VECTOR = ()
-SCATTER_CUTS = (0, 256, 512, 832, 1024)
+EARLY_CHUNKS = 4
+EARLY_PASSES = 3
+ON_VECTOR = (24, 36)
+SCATTER_CUTS = (0, 256, 576, 768, 1024)
 LAST_SPLIT = 48
+GATE_CUTS = (0, 768, 1024)
 
 
 def tile_moe_two_lin_bias_kernel(tc, x_words, x_scales, w, b, gate, offs, dst, out):
     nc = tc.nc
     with ExitStack() as ctx:
         keep = ctx.enter_context(tc.tile_pool(name="keep", bufs=1))
+        late = ctx.enter_context(tc.tile_pool(name="late", bufs=1))
         psum = ctx.enter_context(tc.psum_pool(name="psum", bufs=1))
 
         offs_sb = keep.tile([P, SLOTS // 16], U16, name="offs_sb")
         dst_sb = keep.tile([P, SLOTS // 16], U16, name="dst_sb")
         b_sb = keep.tile([P, E], F32, name="b_sb")
-        gate_sb = keep.tile([P, SLOTS], F32, name="gate_sb")
         y_sb = keep.tile([P, SLOTS], F32, name="y_sb")
         out_sb = keep.tile([P, T], F32, name="out_sb")
-        tok_words = [keep.tile([P, T], I32, name="tok_words%d" % a, align_bytes=64) for a in range(PASSES)]
         slot_words = [keep.tile([P, SLOTS], U32, name="slot_words%d" % a, align_bytes=64) for a in range(PASSES)]
-        tok_scales = keep.tile([P, T], U8, name="tok_scales", align_bytes=64)
-        tok_scales_last = keep.tile([P, T], U8, name="tok_scales_last", align_bytes=64)
         slot_scales = keep.tile([P, SLOTS], U8, name="slot_scales", align_bytes=64)
         slot_scales_last = keep.tile([P, SLOTS], U8, name="slot_scales_last", align_bytes=64)
         acc = [psum.tile([P, C], F32, name="acc%d" % e) for e in range(E)]
 
         first_unit = [sum(CHUNKS[:c]) for c in range(len(CHUNKS))]
-        w_raw = [keep.tile([P, u, PACK, N], F32, name="w_raw%d" % c) for c, u in enumerate(CHUNKS)]
         w_bf = [keep.tile([P, u, N, PACK], BF16, name="w_bf%d" % c, align_bytes=64) for c, u in enumerate(CHUNKS)]
         w_codes = [keep.tile([P, u, N], U32, name="w_codes%d" % c, align_bytes=64) for c, u in enumerate(CHUNKS)]
         w_scales = [keep.tile([P, u, N], U8, name="w_scales%d" % c, align_bytes=64) for c, u in enumerate(CHUNKS)]
         w_rows = w.rearrange("e k n -> (e k) n")
 
-        nc.gpsimd.memset(tok_scales[:].bitcast(I32), 0)
-        nc.gpsimd.memset(tok_scales_last[:].bitcast(I32), 0)
+        unit_bytes = PACK * N * 4
+        words_bytes = T * 4
+        gate_at = (PASSES - EARLY_PASSES) * words_bytes
+        w_at = gate_at + SLOTS * 4
+        late_bytes = w_at + (UNITS - first_unit[EARLY_CHUNKS]) * unit_bytes
+        scales_room = late.tile([P, late_bytes], U8, name="scales_room", offset=0)
+        tok_scales = scales_room[:, 0:T]
+        tok_words = [keep.tile([P, T], I32, name="tok_words%d" % a) for a in range(EARLY_PASSES)]
+        w_raw = [keep.tile([P, CHUNKS[c], PACK, N], F32, name="w_raw%d" % c) for c in range(EARLY_CHUNKS)]
+
+        nc.gpsimd.memset(tok_scales.bitcast(I32), 0)
+        nc.gpsimd.memset(slot_scales_last[:].bitcast(I32), 0)
         nc.gpsimd.memset(out_sb[:], 0.0)
 
         def load_scales(q):
             nc.sync.dma_start(
-                out=tok_scales[32 * q : 32 * q + 16, :].bitcast(I32),
-                in_=x_scales[0:4, 4 * q : 4 * q + 4, :].bitcast(I32),
-            )
-
-        def load_scales_last(q):
-            nc.sync.dma_start(
-                out=tok_scales_last[32 * q : 32 * q + 4, :].bitcast(I32),
-                in_=x_scales[4, 4 * q : 4 * q + 4, :].bitcast(I32),
+                out=tok_scales[32 * q : 32 * q + 4 * PASSES, :].bitcast(I32),
+                in_=x_scales[:, 4 * q : 4 * q + 4, :].bitcast(I32),
             )
 
         def load_tokens(a):
@@ -79,26 +82,9 @@ def tile_moe_two_lin_bias_kernel(tc, x_words, x_scales, w, b, gate, offs, dst, o
                 in_=rows.rearrange("(u p j) n -> p u (j n)", p=P, j=PACK),
             )
 
-        nc.sync.dma_start(offs_sb[:], offs)
-        load_tokens(0)
-        load_w(0)
-        for q in range(4):
-            load_scales(q)
-        load_tokens(1)
-        load_w(1)
-        load_tokens(2)
-        load_w(2)
-        for q in range(4):
-            load_scales_last(q)
-        load_tokens(3)
-        load_w(3)
-        load_tokens(4)
-        load_w(4)
-        nc.sync.dma_start(dst_sb[:], dst)
-        nc.sync.dma_start(out=b_sb[:], in_=b)
-        nc.sync.dma_start(out=gate_sb[:], in_=gate)
-        for c in range(PASSES, len(CHUNKS)):
-            load_w(c)
+        def load_gate(g):
+            cols = slice(GATE_CUTS[g], GATE_CUTS[g + 1])
+            nc.sync.dma_start(out=gate_sb[:, cols], in_=gate[:, cols])
 
         def gather_words(a):
             nc.vector.tensor_copy(slot_words[a][:], tok_words[a][:].bitcast(U32).indirect(offs_sb[:]))
@@ -152,30 +138,75 @@ def tile_moe_two_lin_bias_kernel(tc, x_words, x_scales, w, b, gate, offs, dst, o
         def scatter(s0, s1):
             nc.vector.tensor_copy(out_sb[:].indirect(dst_sb[:, s0 // 16 : s1 // 16]), y_sb[:, s0:s1])
 
+        load_tokens(0)
+        nc.sync.dma_start(offs_sb[:], offs)
+        load_w(0)
+        for q in range(4):
+            load_scales(q)
+        load_tokens(1)
+        load_w(1)
+        load_tokens(2)
+        nc.sync.dma_start(dst_sb[:], dst)
+        nc.sync.dma_start(out=b_sb[:], in_=b)
+        load_w(2)
+        load_w(3)
+
         gather_words(0)
-        nc.vector.tensor_copy(slot_scales[:], tok_scales[:].indirect(offs_sb[:]))
-        for a in range(1, PASSES):
-            round_chunk(a - 1)
-            gather_words(a)
-            if a == 2:
-                nc.vector.tensor_copy(slot_scales_last[:], tok_scales_last[:].indirect(offs_sb[:]))
-            quantize_chunk(a - 1)
+        nc.vector.tensor_copy(slot_scales[:], tok_scales.indirect(offs_sb[:]))
+        nc.sync.dma_start(out=slot_scales_last[0 : P - 16, :].bitcast(I32), in_=slot_scales[16:P, :].bitcast(I32))
+
+        for a in range(EARLY_PASSES, PASSES):
+            at = (a - EARLY_PASSES) * words_bytes
+            tok_words.append(late.tile([P, T], I32, name="tok_words%d" % a, offset=at))
+        gate_sb = late.tile([P, SLOTS], F32, name="gate_sb", offset=gate_at)
+        for c in range(EARLY_CHUNKS, len(CHUNKS)):
+            at = w_at + (first_unit[c] - first_unit[EARLY_CHUNKS]) * unit_bytes
+            w_raw.append(late.tile([P, CHUNKS[c], PACK, N], F32, name="w_raw%d" % c, offset=at))
+        load_tokens(3)
+        load_w(4)
+        load_w(5)
+        load_tokens(4)
+        load_w(6)
+        load_gate(0)
+        for c in range(7, len(CHUNKS)):
+            load_w(c)
+        load_gate(1)
+
+        round_chunk(0)
+        quantize_chunk(0)
+        gather_words(1)
+        round_chunk(1)
+        gather_words(2)
+        quantize_chunk(1)
+        round_chunk(2)
+        round_chunk(3)
+        quantize_chunk(2)
+        gather_words(3)
+        quantize_chunk(3)
+        round_chunk(4)
+        round_chunk(5)
+        quantize_chunk(4)
+        gather_words(4)
+        quantize_chunk(5)
 
         done_units = 0
         done_experts = 0
         done_cuts = 0
-        for c in range(PASSES - 1, len(CHUNKS) + 1):
+        for c in range(6, len(CHUNKS) + 1):
             if c < len(CHUNKS):
                 round_chunk(c)
             ready_units = first_unit[c] if c < len(CHUNKS) else UNITS
             for unit in range(done_units, ready_units):
                 multiply(unit)
             done_units = ready_units
+            ready_experts = done_units // PASSES
+            if ready_experts == E - 1:
+                ready_experts = E - 2
+            for e in range(done_experts, ready_experts):
+                finish_expert(e)
+            done_experts = ready_experts
             if c < len(CHUNKS):
                 quantize_chunk(c)
-            for e in range(done_experts, done_units // PASSES):
-                finish_expert(e)
-            done_experts = done_units // PASSES
             while done_cuts + 1 < len(SCATTER_CUTS) and SCATTER_CUTS[done_cuts + 1] <= done_experts * C:
                 scatter(SCATTER_CUTS[done_cuts], SCATTER_CUTS[done_cuts + 1])
                 done_cuts += 1

@@ -1,6 +1,7 @@
 from contextlib import ExitStack
 
 import concourse.mybir as mybir
+from concourse.masks import make_identity
 
 K, T, E, C, N = 2560, 1536, 8, 128, 128
 SLOTS = E * C
@@ -15,18 +16,20 @@ U8 = mybir.dt.uint8
 FP8X4 = mybir.dt.float8_e4m3fn_x4
 ADD = mybir.AluOpType.add
 MULT = mybir.AluOpType.mult
+COPY = mybir.ActivationFunctionType.Copy
 
 P = 128
 PACK = 4
 PASSES = K // (P * PACK)
 UNITS = E * PASSES
 CHUNKS = [2] * 19 + [1, 1]
-EARLY_CHUNKS = 4
-EARLY_PASSES = 3
-ON_VECTOR = (24, 36)
-SCATTER_CUTS = (0, 256, 576, 768, 1024)
+ON_VECTOR = (25, 37)
 LAST_SPLIT = 48
-GATE_CUTS = (0, 768, 1024)
+BANK = 512
+ACC_BANKS = 5
+EARLY_PASSES = 2
+EARLY_CHUNKS = 2
+FINISH_AFTER = (5, 6, 9, 11, 13, 15, 20)
 
 
 def tile_moe_two_lin_bias_kernel(tc, x_words, x_scales, w, b, gate, offs, dst, out):
@@ -35,16 +38,20 @@ def tile_moe_two_lin_bias_kernel(tc, x_words, x_scales, w, b, gate, offs, dst, o
         keep = ctx.enter_context(tc.tile_pool(name="keep", bufs=1))
         late = ctx.enter_context(tc.tile_pool(name="late", bufs=1))
         psum = ctx.enter_context(tc.psum_pool(name="psum", bufs=1))
+        psum_acc = ctx.enter_context(tc.psum_pool(name="psum_acc", bufs=ACC_BANKS))
 
         offs_sb = keep.tile([P, SLOTS // 16], U16, name="offs_sb")
         dst_sb = keep.tile([P, SLOTS // 16], U16, name="dst_sb")
-        b_sb = keep.tile([P, E], F32, name="b_sb")
-        y_sb = keep.tile([P, SLOTS], F32, name="y_sb")
+        ident = keep.tile([P, P], F32, name="ident")
+        gate_cols = keep.tile([P, E], F32, name="gate_cols")
+        gate_sb = keep.tile([P, SLOTS], F32, name="gate_sb")
+        gated_bias = keep.tile([P, SLOTS], F32, name="gated_bias")
         out_sb = keep.tile([P, T], F32, name="out_sb")
+        tok_scales = keep.tile([P, T], U8, name="tok_scales")
+        tok_words = [keep.tile([P, T], I32, name="tok_words%d" % a) for a in range(EARLY_PASSES)]
         slot_words = [keep.tile([P, SLOTS], U32, name="slot_words%d" % a, align_bytes=64) for a in range(PASSES)]
         slot_scales = keep.tile([P, SLOTS], U8, name="slot_scales", align_bytes=64)
         slot_scales_last = keep.tile([P, SLOTS], U8, name="slot_scales_last", align_bytes=64)
-        acc = [psum.tile([P, C], F32, name="acc%d" % e) for e in range(E)]
 
         first_unit = [sum(CHUNKS[:c]) for c in range(len(CHUNKS))]
         w_bf = [keep.tile([P, u, N, PACK], BF16, name="w_bf%d" % c, align_bytes=64) for c, u in enumerate(CHUNKS)]
@@ -54,17 +61,20 @@ def tile_moe_two_lin_bias_kernel(tc, x_words, x_scales, w, b, gate, offs, dst, o
 
         unit_bytes = PACK * N * 4
         words_bytes = T * 4
-        gate_at = (PASSES - EARLY_PASSES) * words_bytes
-        w_at = gate_at + SLOTS * 4
-        late_bytes = w_at + (UNITS - first_unit[EARLY_CHUNKS]) * unit_bytes
-        scales_room = late.tile([P, late_bytes], U8, name="scales_room", offset=0)
-        tok_scales = scales_room[:, 0:T]
-        tok_words = [keep.tile([P, T], I32, name="tok_words%d" % a) for a in range(EARLY_PASSES)]
+        b_at = (PASSES - EARLY_PASSES) * words_bytes
+        w_at = b_at + E * 4
+        gate_room = late.tile([P, (w_at + (UNITS - first_unit[EARLY_CHUNKS]) * unit_bytes) // 4], F32, name="gate_room", offset=0)
+        gate_rows = gate_room[:, 0:C]
         w_raw = [keep.tile([P, CHUNKS[c], PACK, N], F32, name="w_raw%d" % c) for c in range(EARLY_CHUNKS)]
 
-        nc.gpsimd.memset(tok_scales.bitcast(I32), 0)
-        nc.gpsimd.memset(slot_scales_last[:].bitcast(I32), 0)
-        nc.gpsimd.memset(out_sb[:], 0.0)
+        nc.gpsimd.memset(gate_rows, 0.0)
+        nc.vector.memset(tok_scales[:].bitcast(I32), 0)
+        nc.vector.memset(slot_scales_last[:].bitcast(I32), 0)
+        nc.vector.memset(out_sb[:], 0.0)
+        make_identity(nc, ident[:])
+
+        def raw_at(c):
+            return w_at + (first_unit[c] - first_unit[EARLY_CHUNKS]) * unit_bytes
 
         def load_scales(q):
             nc.sync.dma_start(
@@ -82,12 +92,26 @@ def tile_moe_two_lin_bias_kernel(tc, x_words, x_scales, w, b, gate, offs, dst, o
                 in_=rows.rearrange("(u p j) n -> p u (j n)", p=P, j=PACK),
             )
 
-        def load_gate(g):
-            cols = slice(GATE_CUTS[g], GATE_CUTS[g + 1])
-            nc.sync.dma_start(out=gate_sb[:, cols], in_=gate[:, cols])
+        def spread_gate():
+            nc.scalar.copy(out=gate_cols[:], in_=turned[:, 0:E])
+            for h in range(SLOTS // BANK):
+                spread = psum.tile([P, BANK], F32, name="spread%d" % h)
+                for i in range(BANK // C):
+                    e = h * (BANK // C) + i
+                    nc.tensor.transpose(
+                        spread[:, i * C : (i + 1) * C], gate_cols[:, e : e + 1].to_broadcast([P, P]), ident[:]
+                    )
+                nc.scalar.copy(out=gate_sb[:, h * BANK : (h + 1) * BANK], in_=spread[:])
+            for e in range(E):
+                cols = slice(e * C, (e + 1) * C)
+                nc.scalar.activation(out=gated_bias[:, cols], in_=gate_sb[:, cols], func=COPY, scale=b_sb[:, e : e + 1])
 
         def gather_words(a):
             nc.vector.tensor_copy(slot_words[a][:], tok_words[a][:].bitcast(U32).indirect(offs_sb[:]))
+
+        def gather_scales():
+            nc.vector.tensor_copy(slot_scales[:], tok_scales[:].indirect(offs_sb[:]))
+            nc.scalar.dma_start(out=slot_scales_last[0 : P - 16, :].bitcast(I32), in_=slot_scales[16:P, :].bitcast(I32))
 
         def round_cols(engine, c, i, n0, n1):
             src = w_raw[c][:, i, :, n0:n1].rearrange("p j (g m) -> p g j m", m=4)
@@ -98,8 +122,14 @@ def tile_moe_two_lin_bias_kernel(tc, x_words, x_scales, w, b, gate, offs, dst, o
                 nc.scalar.copy(out=tgt, in_=src)
 
         def round_chunk(c):
-            for i in range(CHUNKS[c]):
-                unit = first_unit[c] + i
+            units = range(first_unit[c], first_unit[c] + CHUNKS[c])
+            if CHUNKS[c] > 1 and not any(unit in ON_VECTOR for unit in units):
+                nc.scalar.copy(
+                    out=w_bf[c][:].rearrange("p u (g m) j -> p u g j m", m=4),
+                    in_=w_raw[c][:].rearrange("p u j (g m) -> p u g j m", m=4),
+                )
+                return
+            for i, unit in enumerate(units):
                 if unit == UNITS - 1:
                     round_cols("scalar", c, i, 0, LAST_SPLIT)
                     round_cols("vector", c, i, LAST_SPLIT, N)
@@ -113,14 +143,14 @@ def tile_moe_two_lin_bias_kernel(tc, x_words, x_scales, w, b, gate, offs, dst, o
                 in_=w_bf[c][:].rearrange("p u n j -> p (u n j)"),
             )
 
-        def multiply(unit):
+        def multiply(unit, acc):
             e, a = divmod(unit, PASSES)
             c = max(cc for cc in range(len(CHUNKS)) if first_unit[cc] <= unit)
             i = unit - first_unit[c]
             cols = slice(e * C, (e + 1) * C)
             rhs_scale = slot_scales[4 * a :, cols] if a < 4 else slot_scales_last[:, cols]
             nc.tensor.matmul_mx(
-                out=acc[e][:],
+                out=acc[:],
                 lhsT=w_codes[c][:, i, :].bitcast(FP8X4),
                 lhsT_scale=w_scales[c][:, i, :],
                 rhs=slot_words[a][:, cols].bitcast(FP8X4),
@@ -129,86 +159,76 @@ def tile_moe_two_lin_bias_kernel(tc, x_words, x_scales, w, b, gate, offs, dst, o
                 stop=(a == PASSES - 1),
             )
 
-        def finish_expert(e):
-            cols = slice(e * C, (e + 1) * C)
-            nc.vector.scalar_tensor_tensor(
-                out=y_sb[:, cols], in0=acc[e][:], scalar=b_sb[:, e : e + 1], in1=gate_sb[:, cols], op0=ADD, op1=MULT
-            )
+        def gate_sums(e, acc):
+            if e < E - 1:
+                gated = late.tile([P, C], F32, name="gated%d" % e, offset=raw_at(FINISH_AFTER[e]))
+            else:
+                gated = keep.tile([P, C], F32, name="gated%d" % e)
+            nc.vector.tensor_tensor(out=gated[:], in0=acc[:], in1=gate_sb[:, e * C : (e + 1) * C], op=MULT)
+            return gated
 
-        def scatter(s0, s1):
-            nc.vector.tensor_copy(out_sb[:].indirect(dst_sb[:, s0 // 16 : s1 // 16]), y_sb[:, s0:s1])
+        def scatter(e, gated):
+            places = dst_sb[:, e * C // 16 : (e + 1) * C // 16]
+            nc.vector.tensor_tensor(out_sb[:].indirect(places), gated[:], gated_bias[:, e * C : (e + 1) * C], ADD)
 
+        nc.scalar.dma_start(out=gate_rows[0:E, :], in_=gate[0, :].rearrange("(e c) -> e c", c=C))
         load_tokens(0)
         nc.sync.dma_start(offs_sb[:], offs)
+        load_tokens(1)
         load_w(0)
+        load_w(1)
         for q in range(4):
             load_scales(q)
-        load_tokens(1)
-        load_w(1)
-        load_tokens(2)
         nc.sync.dma_start(dst_sb[:], dst)
-        nc.sync.dma_start(out=b_sb[:], in_=b)
-        load_w(2)
-        load_w(3)
-
-        gather_words(0)
-        nc.vector.tensor_copy(slot_scales[:], tok_scales.indirect(offs_sb[:]))
-        nc.sync.dma_start(out=slot_scales_last[0 : P - 16, :].bitcast(I32), in_=slot_scales[16:P, :].bitcast(I32))
+        turned = psum.tile([P, P], F32, name="turned")
+        nc.tensor.transpose(turned[:], gate_rows, ident[:])
 
         for a in range(EARLY_PASSES, PASSES):
             at = (a - EARLY_PASSES) * words_bytes
             tok_words.append(late.tile([P, T], I32, name="tok_words%d" % a, offset=at))
-        gate_sb = late.tile([P, SLOTS], F32, name="gate_sb", offset=gate_at)
+        b_sb = late.tile([P, E], F32, name="b_sb", offset=b_at)
         for c in range(EARLY_CHUNKS, len(CHUNKS)):
-            at = w_at + (first_unit[c] - first_unit[EARLY_CHUNKS]) * unit_bytes
-            w_raw.append(late.tile([P, CHUNKS[c], PACK, N], F32, name="w_raw%d" % c, offset=at))
+            w_raw.append(late.tile([P, CHUNKS[c], PACK, N], F32, name="w_raw%d" % c, offset=raw_at(c)))
+        nc.scalar.dma_start(out=b_sb[:], in_=b)
+        load_w(2)
+        load_tokens(2)
+        load_w(3)
         load_tokens(3)
         load_w(4)
-        load_w(5)
         load_tokens(4)
-        load_w(6)
-        load_gate(0)
-        for c in range(7, len(CHUNKS)):
+        for c in range(5, len(CHUNKS)):
             load_w(c)
-        load_gate(1)
 
-        round_chunk(0)
-        quantize_chunk(0)
+        spread_gate()
+        gather_words(0)
         gather_words(1)
+        round_chunk(0)
         round_chunk(1)
-        gather_words(2)
+        quantize_chunk(0)
+        gather_scales()
         quantize_chunk(1)
-        round_chunk(2)
-        round_chunk(3)
-        quantize_chunk(2)
-        gather_words(3)
-        quantize_chunk(3)
-        round_chunk(4)
-        round_chunk(5)
-        quantize_chunk(4)
-        gather_words(4)
-        quantize_chunk(5)
+        for c in range(2, PASSES):
+            round_chunk(c)
+            quantize_chunk(c)
+            gather_words(c)
 
-        done_units = 0
-        done_experts = 0
-        done_cuts = 0
-        for c in range(6, len(CHUNKS) + 1):
-            if c < len(CHUNKS):
-                round_chunk(c)
-            ready_units = first_unit[c] if c < len(CHUNKS) else UNITS
-            for unit in range(done_units, ready_units):
-                multiply(unit)
-            done_units = ready_units
-            ready_experts = done_units // PASSES
-            if ready_experts == E - 1:
-                ready_experts = E - 2
-            for e in range(done_experts, ready_experts):
-                finish_expert(e)
-            done_experts = ready_experts
-            if c < len(CHUNKS):
-                quantize_chunk(c)
-            while done_cuts + 1 < len(SCATTER_CUTS) and SCATTER_CUTS[done_cuts + 1] <= done_experts * C:
-                scatter(SCATTER_CUTS[done_cuts], SCATTER_CUTS[done_cuts + 1])
-                done_cuts += 1
+        accs = {}
+
+        def multiply_units(u0, u1):
+            for unit in range(u0, u1):
+                e = unit // PASSES
+                if e not in accs:
+                    accs[e] = psum_acc.tile([P, C], F32, name="acc")
+                multiply(unit, accs[e])
+
+        multiply_units(0, first_unit[PASSES])
+        for c in range(PASSES, len(CHUNKS)):
+            round_chunk(c)
+            due = [(e, gate_sums(e, accs[e])) for e in range(E - 1) if FINISH_AFTER[e] == c]
+            quantize_chunk(c)
+            multiply_units(first_unit[c], first_unit[c] + CHUNKS[c])
+            for e, gated in due:
+                scatter(e, gated)
+        scatter(E - 1, gate_sums(E - 1, accs[E - 1]))
 
         nc.sync.dma_start(out=out, in_=out_sb[:])

@@ -1,7 +1,6 @@
 from contextlib import ExitStack
 
 import concourse.mybir as mybir
-from concourse.masks import make_identity
 
 K, T, E, C, N = 2560, 1536, 8, 128, 128
 SLOTS = E * C
@@ -23,13 +22,13 @@ PACK = 4
 PASSES = K // (P * PACK)
 UNITS = E * PASSES
 CHUNKS = [2] * 19 + [1, 1]
-ON_VECTOR = (25, 37)
+ON_VECTOR = (19, 25, 31, 37)
 LAST_SPLIT = 48
 BANK = 512
 ACC_BANKS = 5
-EARLY_PASSES = 2
-EARLY_CHUNKS = 2
-FINISH_AFTER = (5, 6, 9, 11, 13, 15, 20)
+EARLY_PASSES = 1
+EARLY_CHUNKS = 0
+FINISH_AFTER = (4, 6, 9, 10, 13, 15, 20)
 
 
 def tile_moe_two_lin_bias_kernel(tc, x_words, x_scales, w, b, gate, offs, dst, out):
@@ -37,6 +36,7 @@ def tile_moe_two_lin_bias_kernel(tc, x_words, x_scales, w, b, gate, offs, dst, o
     with ExitStack() as ctx:
         keep = ctx.enter_context(tc.tile_pool(name="keep", bufs=1))
         late = ctx.enter_context(tc.tile_pool(name="late", bufs=1))
+        turns = ctx.enter_context(tc.tile_pool(name="turns", bufs=1))
         psum = ctx.enter_context(tc.psum_pool(name="psum", bufs=1))
         psum_acc = ctx.enter_context(tc.psum_pool(name="psum_acc", bufs=ACC_BANKS))
 
@@ -47,9 +47,10 @@ def tile_moe_two_lin_bias_kernel(tc, x_words, x_scales, w, b, gate, offs, dst, o
         gate_sb = keep.tile([P, SLOTS], F32, name="gate_sb")
         gated_bias = keep.tile([P, SLOTS], F32, name="gated_bias")
         out_sb = keep.tile([P, T], F32, name="out_sb")
-        tok_scales = keep.tile([P, T], U8, name="tok_scales")
+        gate_rows = keep.tile([P, C], F32, name="gate_rows")
+        tok_scales = turns.tile([P, T], U8, name="tok_scales", offset=0, align_bytes=64)
         tok_words = [keep.tile([P, T], I32, name="tok_words%d" % a) for a in range(EARLY_PASSES)]
-        slot_words = [keep.tile([P, SLOTS], U32, name="slot_words%d" % a, align_bytes=64) for a in range(PASSES)]
+        slot_words = {a: keep.tile([P, SLOTS], U32, name="slot_words%d" % a, align_bytes=64) for a in range(1, PASSES)}
         slot_scales = keep.tile([P, SLOTS], U8, name="slot_scales", align_bytes=64)
         slot_scales_last = keep.tile([P, SLOTS], U8, name="slot_scales_last", align_bytes=64)
 
@@ -63,23 +64,31 @@ def tile_moe_two_lin_bias_kernel(tc, x_words, x_scales, w, b, gate, offs, dst, o
         words_bytes = T * 4
         b_at = (PASSES - EARLY_PASSES) * words_bytes
         w_at = b_at + E * 4
-        gate_room = late.tile([P, (w_at + (UNITS - first_unit[EARLY_CHUNKS]) * unit_bytes) // 4], F32, name="gate_room", offset=0)
-        gate_rows = gate_room[:, 0:C]
+        zero_room = late.tile([P, (w_at + (UNITS - first_unit[EARLY_CHUNKS]) * unit_bytes) // 4], F32, name="zero_room", offset=0)
         w_raw = [keep.tile([P, CHUNKS[c], PACK, N], F32, name="w_raw%d" % c) for c in range(EARLY_CHUNKS)]
 
-        nc.gpsimd.memset(gate_rows, 0.0)
-        nc.vector.memset(tok_scales[:].bitcast(I32), 0)
+        nc.gpsimd.memset(tok_scales[:].bitcast(I32), 0)
+        nc.gpsimd.memset(zero_room[:, 0:P], 0.0)
+        nc.gpsimd.affine_select(
+            out=ident[:],
+            in_=zero_room[:, 0:P],
+            compare_op=mybir.AluOpType.not_equal,
+            fill=1.0,
+            base=0,
+            pattern=[[-1, P]],
+            channel_multiplier=1,
+        )
+        nc.vector.memset(gate_rows[:], 0.0)
         nc.vector.memset(slot_scales_last[:].bitcast(I32), 0)
         nc.vector.memset(out_sb[:], 0.0)
-        make_identity(nc, ident[:])
 
         def raw_at(c):
             return w_at + (first_unit[c] - first_unit[EARLY_CHUNKS]) * unit_bytes
 
         def load_scales(q):
-            nc.sync.dma_start(
-                out=tok_scales[32 * q : 32 * q + 4 * PASSES, :].bitcast(I32),
-                in_=x_scales[:, 4 * q : 4 * q + 4, :].bitcast(I32),
+            nc.scalar.dma_start(
+                out=tok_scales[32 * q : 32 * q + 16, :].bitcast(I32),
+                in_=x_scales[0:4, 4 * q : 4 * q + 4, :].bitcast(I32),
             )
 
         def load_tokens(a):
@@ -93,6 +102,8 @@ def tile_moe_two_lin_bias_kernel(tc, x_words, x_scales, w, b, gate, offs, dst, o
             )
 
         def spread_gate():
+            turned = psum.tile([P, P], F32, name="turned")
+            nc.tensor.transpose(turned[:], gate_rows[:], ident[:])
             nc.scalar.copy(out=gate_cols[:], in_=turned[:, 0:E])
             for h in range(SLOTS // BANK):
                 spread = psum.tile([P, BANK], F32, name="spread%d" % h)
@@ -111,7 +122,11 @@ def tile_moe_two_lin_bias_kernel(tc, x_words, x_scales, w, b, gate, offs, dst, o
 
         def gather_scales():
             nc.vector.tensor_copy(slot_scales[:], tok_scales[:].indirect(offs_sb[:]))
-            nc.scalar.dma_start(out=slot_scales_last[0 : P - 16, :].bitcast(I32), in_=slot_scales[16:P, :].bitcast(I32))
+            for q in range(4):
+                nc.gpsimd.dma_start(
+                    out=slot_scales_last[32 * q : 32 * q + 4, :].bitcast(I32),
+                    in_=slot_scales[16 + 4 * q : 20 + 4 * q, :].bitcast(I32),
+                )
 
         def round_cols(engine, c, i, n0, n1):
             src = w_raw[c][:, i, :, n0:n1].rearrange("p j (g m) -> p g j m", m=4)
@@ -171,17 +186,13 @@ def tile_moe_two_lin_bias_kernel(tc, x_words, x_scales, w, b, gate, offs, dst, o
             places = dst_sb[:, e * C // 16 : (e + 1) * C // 16]
             nc.vector.tensor_tensor(out_sb[:].indirect(places), gated[:], gated_bias[:, e * C : (e + 1) * C], ADD)
 
-        nc.scalar.dma_start(out=gate_rows[0:E, :], in_=gate[0, :].rearrange("(e c) -> e c", c=C))
-        load_tokens(0)
         nc.sync.dma_start(offs_sb[:], offs)
-        load_tokens(1)
-        load_w(0)
-        load_w(1)
+        nc.sync.dma_start(dst_sb[:], dst)
+        load_tokens(0)
         for q in range(4):
             load_scales(q)
-        nc.sync.dma_start(dst_sb[:], dst)
-        turned = psum.tile([P, P], F32, name="turned")
-        nc.tensor.transpose(turned[:], gate_rows, ident[:])
+        nc.scalar.dma_start(out=tok_scales[16:32, :].bitcast(I32), in_=x_scales[PASSES - 1].bitcast(I32))
+        nc.scalar.dma_start(out=gate_rows[0:E, :], in_=gate[0, :].rearrange("(e c) -> e c", c=C))
 
         for a in range(EARLY_PASSES, PASSES):
             at = (a - EARLY_PASSES) * words_bytes
@@ -190,27 +201,32 @@ def tile_moe_two_lin_bias_kernel(tc, x_words, x_scales, w, b, gate, offs, dst, o
         for c in range(EARLY_CHUNKS, len(CHUNKS)):
             w_raw.append(late.tile([P, CHUNKS[c], PACK, N], F32, name="w_raw%d" % c, offset=raw_at(c)))
         nc.scalar.dma_start(out=b_sb[:], in_=b)
-        load_w(2)
+        load_w(0)
+        load_tokens(1)
+        load_w(1)
         load_tokens(2)
-        load_w(3)
         load_tokens(3)
-        load_w(4)
+        load_w(2)
         load_tokens(4)
-        for c in range(5, len(CHUNKS)):
+        for c in range(3, len(CHUNKS)):
             load_w(c)
 
-        spread_gate()
-        gather_words(0)
-        gather_words(1)
-        round_chunk(0)
-        round_chunk(1)
-        quantize_chunk(0)
         gather_scales()
+        slot_words[0] = turns.tile([P, SLOTS], U32, name="slot_words0", offset=0, align_bytes=64)
+        gather_words(0)
+        spread_gate()
+        round_chunk(0)
+        gather_words(1)
+        quantize_chunk(0)
+        round_chunk(1)
+        gather_words(2)
         quantize_chunk(1)
-        for c in range(2, PASSES):
-            round_chunk(c)
-            quantize_chunk(c)
-            gather_words(c)
+        gather_words(3)
+        round_chunk(2)
+        quantize_chunk(2)
+        gather_words(4)
+        round_chunk(3)
+        quantize_chunk(3)
 
         accs = {}
 
@@ -221,8 +237,8 @@ def tile_moe_two_lin_bias_kernel(tc, x_words, x_scales, w, b, gate, offs, dst, o
                     accs[e] = psum_acc.tile([P, C], F32, name="acc")
                 multiply(unit, accs[e])
 
-        multiply_units(0, first_unit[PASSES])
-        for c in range(PASSES, len(CHUNKS)):
+        multiply_units(0, first_unit[4])
+        for c in range(4, len(CHUNKS)):
             round_chunk(c)
             due = [(e, gate_sums(e, accs[e])) for e in range(E - 1) if FINISH_AFTER[e] == c]
             quantize_chunk(c)

@@ -22,13 +22,13 @@ PACK = 4
 PASSES = K // (P * PACK)
 UNITS = E * PASSES
 CHUNKS = [2] * 19 + [1, 1]
-ON_VECTOR = (19, 25, 31, 37)
+ON_VECTOR = (19, 27, 29, 37)
 LAST_SPLIT = 48
 BANK = 512
 ACC_BANKS = 5
 EARLY_PASSES = 1
-EARLY_CHUNKS = 0
-FINISH_AFTER = (4, 6, 9, 10, 13, 15, 20)
+LOADS = [2] * 3 + [4] * 6 + [2] * 4 + [1, 1]
+FINISH_AFTER = (3, 4, 5, 6, 8, 9, 14)
 
 
 def tile_moe_two_lin_bias_kernel(tc, x_words, x_scales, w, b, gate, offs, dst, out):
@@ -64,8 +64,9 @@ def tile_moe_two_lin_bias_kernel(tc, x_words, x_scales, w, b, gate, offs, dst, o
         words_bytes = T * 4
         b_at = (PASSES - EARLY_PASSES) * words_bytes
         w_at = b_at + E * 4
-        zero_room = late.tile([P, (w_at + (UNITS - first_unit[EARLY_CHUNKS]) * unit_bytes) // 4], F32, name="zero_room", offset=0)
-        w_raw = [keep.tile([P, CHUNKS[c], PACK, N], F32, name="w_raw%d" % c) for c in range(EARLY_CHUNKS)]
+        load_first = [sum(LOADS[:d]) for d in range(len(LOADS))]
+        load_of = [d for d, u in enumerate(LOADS) for i in range(u)]
+        zero_room = late.tile([P, (w_at + UNITS * unit_bytes) // 4], F32, name="zero_room", offset=0)
 
         nc.gpsimd.memset(tok_scales[:].bitcast(I32), 0)
         nc.gpsimd.memset(zero_room[:, 0:P], 0.0)
@@ -82,8 +83,13 @@ def tile_moe_two_lin_bias_kernel(tc, x_words, x_scales, w, b, gate, offs, dst, o
         nc.vector.memset(slot_scales_last[:].bitcast(I32), 0)
         nc.vector.memset(out_sb[:], 0.0)
 
-        def raw_at(c):
-            return w_at + (first_unit[c] - first_unit[EARLY_CHUNKS]) * unit_bytes
+        def raw_at(d):
+            return w_at + load_first[d] * unit_bytes
+
+        def raw_units(c):
+            d = load_of[first_unit[c]]
+            i = first_unit[c] - load_first[d]
+            return w_raw[d][:, i : i + CHUNKS[c]]
 
         def load_scales(q):
             nc.scalar.dma_start(
@@ -95,7 +101,7 @@ def tile_moe_two_lin_bias_kernel(tc, x_words, x_scales, w, b, gate, offs, dst, o
             nc.sync.dma_start(out=tok_words[a][:], in_=x_words[a].rearrange("p t r -> p (t r)").bitcast(I32))
 
         def load_w(c):
-            rows = w_rows[first_unit[c] * P * PACK : (first_unit[c] + CHUNKS[c]) * P * PACK, :]
+            rows = w_rows[load_first[c] * P * PACK : (load_first[c] + LOADS[c]) * P * PACK, :]
             nc.sync.dma_start(
                 out=w_raw[c][:].rearrange("p u j n -> p u (j n)"),
                 in_=rows.rearrange("(u p j) n -> p u (j n)", p=P, j=PACK),
@@ -129,7 +135,7 @@ def tile_moe_two_lin_bias_kernel(tc, x_words, x_scales, w, b, gate, offs, dst, o
                 )
 
         def round_cols(engine, c, i, n0, n1):
-            src = w_raw[c][:, i, :, n0:n1].rearrange("p j (g m) -> p g j m", m=4)
+            src = raw_units(c)[:, i, :, n0:n1].rearrange("p j (g m) -> p g j m", m=4)
             tgt = w_bf[c][:, i, n0:n1, :].rearrange("p (g m) j -> p g j m", m=4)
             if engine == "vector":
                 nc.vector.tensor_copy(out=tgt, in_=src)
@@ -141,7 +147,7 @@ def tile_moe_two_lin_bias_kernel(tc, x_words, x_scales, w, b, gate, offs, dst, o
             if CHUNKS[c] > 1 and not any(unit in ON_VECTOR for unit in units):
                 nc.scalar.copy(
                     out=w_bf[c][:].rearrange("p u (g m) j -> p u g j m", m=4),
-                    in_=w_raw[c][:].rearrange("p u j (g m) -> p u g j m", m=4),
+                    in_=raw_units(c).rearrange("p u j (g m) -> p u g j m", m=4),
                 )
                 return
             for i, unit in enumerate(units):
@@ -198,18 +204,17 @@ def tile_moe_two_lin_bias_kernel(tc, x_words, x_scales, w, b, gate, offs, dst, o
             at = (a - EARLY_PASSES) * words_bytes
             tok_words.append(late.tile([P, T], I32, name="tok_words%d" % a, offset=at))
         b_sb = late.tile([P, E], F32, name="b_sb", offset=b_at)
-        for c in range(EARLY_CHUNKS, len(CHUNKS)):
-            w_raw.append(late.tile([P, CHUNKS[c], PACK, N], F32, name="w_raw%d" % c, offset=raw_at(c)))
-        nc.scalar.dma_start(out=b_sb[:], in_=b)
+        w_raw = [late.tile([P, u, PACK, N], F32, name="w_raw%d" % d, offset=raw_at(d)) for d, u in enumerate(LOADS)]
         load_w(0)
         load_tokens(1)
         load_w(1)
+        nc.sync.dma_start(out=b_sb[:], in_=b)
         load_tokens(2)
         load_tokens(3)
         load_w(2)
         load_tokens(4)
-        for c in range(3, len(CHUNKS)):
-            load_w(c)
+        for d in range(3, len(LOADS)):
+            load_w(d)
 
         gather_scales()
         slot_words[0] = turns.tile([P, SLOTS], U32, name="slot_words0", offset=0, align_bytes=64)
@@ -240,7 +245,7 @@ def tile_moe_two_lin_bias_kernel(tc, x_words, x_scales, w, b, gate, offs, dst, o
         multiply_units(0, first_unit[4])
         for c in range(4, len(CHUNKS)):
             round_chunk(c)
-            due = [(e, gate_sums(e, accs[e])) for e in range(E - 1) if FINISH_AFTER[e] == c]
+            due = [(e, gate_sums(e, accs[e])) for e in range(E - 1) if load_first[FINISH_AFTER[e]] + LOADS[FINISH_AFTER[e]] == first_unit[c] + CHUNKS[c]]
             quantize_chunk(c)
             multiply_units(first_unit[c], first_unit[c] + CHUNKS[c])
             for e, gated in due:

@@ -21,14 +21,13 @@ P = 128
 PACK = 4
 PASSES = K // (P * PACK)
 UNITS = E * PASSES
-CHUNKS = [2] * 19 + [1, 1]
-ON_VECTOR = (19, 27, 29, 37)
-LAST_SPLIT = 48
+CHUNKS = [2] * 20
+ON_VECTOR = (25, 37, 39)
 BANK = 512
 ACC_BANKS = 5
-EARLY_PASSES = 1
-LOADS = [2] * 3 + [4] * 6 + [2] * 4 + [1, 1]
-FINISH_AFTER = (3, 4, 5, 6, 8, 9, 14)
+EARLY_PASSES = 0
+LOADS = [2] * 19 + [1, 1]
+FINISH_AFTER = (4, 6, 9, 10, 13, 15, 19)
 
 
 def tile_moe_two_lin_bias_kernel(tc, x_words, x_scales, w, b, gate, offs, dst, out):
@@ -92,7 +91,7 @@ def tile_moe_two_lin_bias_kernel(tc, x_words, x_scales, w, b, gate, offs, dst, o
             return w_raw[d][:, i : i + CHUNKS[c]]
 
         def load_scales(q):
-            nc.scalar.dma_start(
+            nc.sync.dma_start(
                 out=tok_scales[32 * q : 32 * q + 16, :].bitcast(I32),
                 in_=x_scales[0:4, 4 * q : 4 * q + 4, :].bitcast(I32),
             )
@@ -134,28 +133,22 @@ def tile_moe_two_lin_bias_kernel(tc, x_words, x_scales, w, b, gate, offs, dst, o
                     in_=slot_scales[16 + 4 * q : 20 + 4 * q, :].bitcast(I32),
                 )
 
-        def round_cols(engine, c, i, n0, n1):
-            src = raw_units(c)[:, i, :, n0:n1].rearrange("p j (g m) -> p g j m", m=4)
-            tgt = w_bf[c][:, i, n0:n1, :].rearrange("p (g m) j -> p g j m", m=4)
-            if engine == "vector":
-                nc.vector.tensor_copy(out=tgt, in_=src)
-            else:
-                nc.scalar.copy(out=tgt, in_=src)
-
         def round_chunk(c):
             units = range(first_unit[c], first_unit[c] + CHUNKS[c])
-            if CHUNKS[c] > 1 and not any(unit in ON_VECTOR for unit in units):
+            if not any(unit in ON_VECTOR for unit in units):
                 nc.scalar.copy(
                     out=w_bf[c][:].rearrange("p u (g m) j -> p u g j m", m=4),
                     in_=raw_units(c).rearrange("p u j (g m) -> p u g j m", m=4),
                 )
                 return
             for i, unit in enumerate(units):
-                if unit == UNITS - 1:
-                    round_cols("scalar", c, i, 0, LAST_SPLIT)
-                    round_cols("vector", c, i, LAST_SPLIT, N)
+                d = load_of[unit]
+                src = w_raw[d][:, unit - load_first[d]].rearrange("p j (g m) -> p g j m", m=4)
+                tgt = w_bf[c][:, i].rearrange("p (g m) j -> p g j m", m=4)
+                if unit in ON_VECTOR:
+                    nc.vector.tensor_copy(out=tgt, in_=src)
                 else:
-                    round_cols("vector" if unit in ON_VECTOR else "scalar", c, i, 0, N)
+                    nc.scalar.copy(out=tgt, in_=src)
 
         def quantize_chunk(c):
             nc.vector.quantize_mx(
@@ -194,10 +187,9 @@ def tile_moe_two_lin_bias_kernel(tc, x_words, x_scales, w, b, gate, offs, dst, o
 
         nc.sync.dma_start(offs_sb[:], offs)
         nc.sync.dma_start(dst_sb[:], dst)
-        load_tokens(0)
         for q in range(4):
             load_scales(q)
-        nc.scalar.dma_start(out=tok_scales[16:32, :].bitcast(I32), in_=x_scales[PASSES - 1].bitcast(I32))
+        nc.sync.dma_start(out=tok_scales[16:32, :].bitcast(I32), in_=x_scales[PASSES - 1].bitcast(I32))
         nc.scalar.dma_start(out=gate_rows[0:E, :], in_=gate[0, :].rearrange("(e c) -> e c", c=C))
 
         for a in range(EARLY_PASSES, PASSES):
@@ -205,11 +197,12 @@ def tile_moe_two_lin_bias_kernel(tc, x_words, x_scales, w, b, gate, offs, dst, o
             tok_words.append(late.tile([P, T], I32, name="tok_words%d" % a, offset=at))
         b_sb = late.tile([P, E], F32, name="b_sb", offset=b_at)
         w_raw = [late.tile([P, u, PACK, N], F32, name="w_raw%d" % d, offset=raw_at(d)) for d, u in enumerate(LOADS)]
-        load_w(0)
+        load_tokens(0)
         load_tokens(1)
-        load_w(1)
+        load_w(0)
         nc.sync.dma_start(out=b_sb[:], in_=b)
         load_tokens(2)
+        load_w(1)
         load_tokens(3)
         load_w(2)
         load_tokens(4)
@@ -220,11 +213,11 @@ def tile_moe_two_lin_bias_kernel(tc, x_words, x_scales, w, b, gate, offs, dst, o
         slot_words[0] = turns.tile([P, SLOTS], U32, name="slot_words0", offset=0, align_bytes=64)
         gather_words(0)
         spread_gate()
-        round_chunk(0)
         gather_words(1)
+        round_chunk(0)
         quantize_chunk(0)
-        round_chunk(1)
         gather_words(2)
+        round_chunk(1)
         quantize_chunk(1)
         gather_words(3)
         round_chunk(2)
@@ -245,7 +238,7 @@ def tile_moe_two_lin_bias_kernel(tc, x_words, x_scales, w, b, gate, offs, dst, o
         multiply_units(0, first_unit[4])
         for c in range(4, len(CHUNKS)):
             round_chunk(c)
-            due = [(e, gate_sums(e, accs[e])) for e in range(E - 1) if load_first[FINISH_AFTER[e]] + LOADS[FINISH_AFTER[e]] == first_unit[c] + CHUNKS[c]]
+            due = [(e, gate_sums(e, accs[e])) for e in range(E - 1) if (load_first[FINISH_AFTER[e]] + LOADS[FINISH_AFTER[e]] - 1) // 2 == c]
             quantize_chunk(c)
             multiply_units(first_unit[c], first_unit[c] + CHUNKS[c])
             for e, gated in due:

@@ -1,6 +1,7 @@
 from contextlib import ExitStack
 
 import concourse.mybir as mybir
+from concourse.masks import make_identity
 
 K, T, E, C, N = 2560, 1536, 8, 128, 128
 SLOTS = E * C
@@ -21,13 +22,14 @@ P = 128
 PACK = 4
 PASSES = K // (P * PACK)
 UNITS = E * PASSES
-CHUNKS = [2] * 20
+CHUNKS = [2, 4] + [2] * 17
 ON_VECTOR = (25, 37, 39)
 BANK = 512
 ACC_BANKS = 5
-EARLY_PASSES = 0
-LOADS = [2] * 19 + [1, 1]
-FINISH_AFTER = (4, 6, 9, 10, 13, 15, 19)
+EARLY_PASSES = 1
+EARLY_LOADS = 2
+LOADS = [2, 4] + [2] * 16 + [1, 1]
+FINISH_AFTER = (3, 5, 8, 9, 12, 14, 19)
 
 
 def tile_moe_two_lin_bias_kernel(tc, x_words, x_scales, w, b, gate, offs, dst, out):
@@ -35,21 +37,17 @@ def tile_moe_two_lin_bias_kernel(tc, x_words, x_scales, w, b, gate, offs, dst, o
     with ExitStack() as ctx:
         keep = ctx.enter_context(tc.tile_pool(name="keep", bufs=1))
         late = ctx.enter_context(tc.tile_pool(name="late", bufs=1))
-        turns = ctx.enter_context(tc.tile_pool(name="turns", bufs=1))
         psum = ctx.enter_context(tc.psum_pool(name="psum", bufs=1))
         psum_acc = ctx.enter_context(tc.psum_pool(name="psum_acc", bufs=ACC_BANKS))
 
         offs_sb = keep.tile([P, SLOTS // 16], U16, name="offs_sb")
         dst_sb = keep.tile([P, SLOTS // 16], U16, name="dst_sb")
         ident = keep.tile([P, P], F32, name="ident")
-        gate_cols = keep.tile([P, E], F32, name="gate_cols")
         gate_sb = keep.tile([P, SLOTS], F32, name="gate_sb")
         gated_bias = keep.tile([P, SLOTS], F32, name="gated_bias")
         out_sb = keep.tile([P, T], F32, name="out_sb")
-        gate_rows = keep.tile([P, C], F32, name="gate_rows")
-        tok_scales = turns.tile([P, T], U8, name="tok_scales", offset=0, align_bytes=64)
         tok_words = [keep.tile([P, T], I32, name="tok_words%d" % a) for a in range(EARLY_PASSES)]
-        slot_words = {a: keep.tile([P, SLOTS], U32, name="slot_words%d" % a, align_bytes=64) for a in range(1, PASSES)}
+        slot_words = {a: keep.tile([P, SLOTS], U32, name="slot_words%d" % a, align_bytes=64) for a in range(PASSES)}
         slot_scales = keep.tile([P, SLOTS], U8, name="slot_scales", align_bytes=64)
         slot_scales_last = keep.tile([P, SLOTS], U8, name="slot_scales_last", align_bytes=64)
 
@@ -61,26 +59,26 @@ def tile_moe_two_lin_bias_kernel(tc, x_words, x_scales, w, b, gate, offs, dst, o
 
         unit_bytes = PACK * N * 4
         words_bytes = T * 4
-        b_at = (PASSES - EARLY_PASSES) * words_bytes
-        w_at = b_at + E * 4
         load_first = [sum(LOADS[:d]) for d in range(len(LOADS))]
         load_of = [d for d, u in enumerate(LOADS) for i in range(u)]
-        zero_room = late.tile([P, (w_at + UNITS * unit_bytes) // 4], F32, name="zero_room", offset=0)
-
-        nc.gpsimd.memset(tok_scales[:].bitcast(I32), 0)
-        nc.gpsimd.memset(zero_room[:, 0:P], 0.0)
-        nc.gpsimd.affine_select(
-            out=ident[:],
-            in_=zero_room[:, 0:P],
-            compare_op=mybir.AluOpType.not_equal,
-            fill=1.0,
-            base=0,
-            pattern=[[-1, P]],
-            channel_multiplier=1,
+        b_at = 2 * words_bytes
+        gate_at = b_at + 64
+        w_at = gate_at + 64
+        second_at = w_at + load_first[EARLY_LOADS] * unit_bytes
+        last_words_at = w_at + UNITS * unit_bytes
+        words_at = [None, 0, words_bytes, last_words_at, last_words_at + words_bytes]
+        zero_room = late.tile([P, second_at // 4], F32, name="zero_room", offset=0)
+        scale_room = late.tile(
+            [P, last_words_at + 2 * words_bytes - second_at], U8, name="scale_room", offset=second_at, align_bytes=64
         )
-        nc.vector.memset(gate_rows[:], 0.0)
+        tok_scales = scale_room[:, 0:T]
+
+        nc.vector.memset(tok_scales.bitcast(I32), 0)
+        nc.vector.memset(zero_room[:, 0:P], 0.0)
         nc.vector.memset(slot_scales_last[:].bitcast(I32), 0)
-        nc.vector.memset(out_sb[:], 0.0)
+        nc.vector.tensor_copy(out=out_sb[:, 0:P], in_=zero_room[:, 0:P])
+        nc.vector.memset(out_sb[:, P:T], 0.0)
+        make_identity(nc, ident[:])
 
         def raw_at(d):
             return w_at + load_first[d] * unit_bytes
@@ -92,7 +90,7 @@ def tile_moe_two_lin_bias_kernel(tc, x_words, x_scales, w, b, gate, offs, dst, o
 
         def load_scales(q):
             nc.sync.dma_start(
-                out=tok_scales[32 * q : 32 * q + 16, :].bitcast(I32),
+                out=scale_room[32 * q : 32 * q + 16, 0:T].bitcast(I32),
                 in_=x_scales[0:4, 4 * q : 4 * q + 4, :].bitcast(I32),
             )
 
@@ -107,17 +105,16 @@ def tile_moe_two_lin_bias_kernel(tc, x_words, x_scales, w, b, gate, offs, dst, o
             )
 
         def spread_gate():
-            turned = psum.tile([P, P], F32, name="turned")
-            nc.tensor.transpose(turned[:], gate_rows[:], ident[:])
-            nc.scalar.copy(out=gate_cols[:], in_=turned[:, 0:E])
+            per_bank = BANK // P
             for h in range(SLOTS // BANK):
-                spread = psum.tile([P, BANK], F32, name="spread%d" % h)
-                for i in range(BANK // C):
-                    e = h * (BANK // C) + i
-                    nc.tensor.transpose(
-                        spread[:, i * C : (i + 1) * C], gate_cols[:, e : e + 1].to_broadcast([P, P]), ident[:]
-                    )
-                nc.scalar.copy(out=gate_sb[:, h * BANK : (h + 1) * BANK], in_=spread[:])
+                spread = psum.tile([P, per_bank, P], F32, name="spread%d" % h)
+                for i in range(per_bank):
+                    j = h * per_bank + i
+                    nc.tensor.transpose(spread[:, i, :], gate_cols[:, j : j + 1].to_broadcast([P, P]), ident[:])
+                nc.scalar.copy(
+                    out=gate_sb[:].rearrange("n (p j) -> n p j", p=P)[:, :, h * per_bank : (h + 1) * per_bank],
+                    in_=spread[:].rearrange("n j p -> n p j"),
+                )
             for e in range(E):
                 cols = slice(e * C, (e + 1) * C)
                 nc.scalar.activation(out=gated_bias[:, cols], in_=gate_sb[:, cols], func=COPY, scale=b_sb[:, e : e + 1])
@@ -126,9 +123,11 @@ def tile_moe_two_lin_bias_kernel(tc, x_words, x_scales, w, b, gate, offs, dst, o
             nc.vector.tensor_copy(slot_words[a][:], tok_words[a][:].bitcast(U32).indirect(offs_sb[:]))
 
         def gather_scales():
-            nc.vector.tensor_copy(slot_scales[:], tok_scales[:].indirect(offs_sb[:]))
+            nc.vector.tensor_copy(slot_scales[:], tok_scales.indirect(offs_sb[:]))
+
+        def move_last_scales():
             for q in range(4):
-                nc.gpsimd.dma_start(
+                nc.sync.dma_start(
                     out=slot_scales_last[32 * q : 32 * q + 4, :].bitcast(I32),
                     in_=slot_scales[16 + 4 * q : 20 + 4 * q, :].bitcast(I32),
                 )
@@ -186,45 +185,44 @@ def tile_moe_two_lin_bias_kernel(tc, x_words, x_scales, w, b, gate, offs, dst, o
             nc.vector.tensor_tensor(out_sb[:].indirect(places), gated[:], gated_bias[:, e * C : (e + 1) * C], ADD)
 
         nc.sync.dma_start(offs_sb[:], offs)
+        load_tokens(0)
         nc.sync.dma_start(dst_sb[:], dst)
         for q in range(4):
             load_scales(q)
-        nc.sync.dma_start(out=tok_scales[16:32, :].bitcast(I32), in_=x_scales[PASSES - 1].bitcast(I32))
-        nc.scalar.dma_start(out=gate_rows[0:E, :], in_=gate[0, :].rearrange("(e c) -> e c", c=C))
+        nc.sync.dma_start(out=scale_room[16:32, 0:T].bitcast(I32), in_=x_scales[PASSES - 1].bitcast(I32))
 
-        for a in range(EARLY_PASSES, PASSES):
-            at = (a - EARLY_PASSES) * words_bytes
-            tok_words.append(late.tile([P, T], I32, name="tok_words%d" % a, offset=at))
+        for a in range(EARLY_PASSES, 3):
+            tok_words.append(late.tile([P, T], I32, name="tok_words%d" % a, offset=words_at[a]))
         b_sb = late.tile([P, E], F32, name="b_sb", offset=b_at)
-        w_raw = [late.tile([P, u, PACK, N], F32, name="w_raw%d" % d, offset=raw_at(d)) for d, u in enumerate(LOADS)]
-        load_tokens(0)
+        gate_cols = late.tile([P, SLOTS // P], F32, name="gate_cols", offset=gate_at)
+        w_raw = [late.tile([P, u, PACK, N], F32, name="w_raw%d" % d, offset=raw_at(d)) for d, u in enumerate(LOADS[:EARLY_LOADS])]
         load_tokens(1)
         load_w(0)
+        nc.sync.dma_start(out=gate_cols[:], in_=gate[0, :].rearrange("(p j) -> p j", p=P))
         nc.sync.dma_start(out=b_sb[:], in_=b)
         load_tokens(2)
         load_w(1)
-        load_tokens(3)
-        load_w(2)
-        load_tokens(4)
-        for d in range(3, len(LOADS)):
-            load_w(d)
 
-        gather_scales()
-        slot_words[0] = turns.tile([P, SLOTS], U32, name="slot_words0", offset=0, align_bytes=64)
         gather_words(0)
-        spread_gate()
+        gather_scales()
+        move_last_scales()
+        for a in range(3, PASSES):
+            tok_words.append(late.tile([P, T], I32, name="tok_words%d" % a, offset=words_at[a]))
+            load_tokens(a)
+        for d in range(EARLY_LOADS, len(LOADS)):
+            w_raw.append(late.tile([P, LOADS[d], PACK, N], F32, name="w_raw%d" % d, offset=raw_at(d)))
+            load_w(d)
         gather_words(1)
+        spread_gate()
         round_chunk(0)
-        quantize_chunk(0)
         gather_words(2)
+        quantize_chunk(0)
         round_chunk(1)
-        quantize_chunk(1)
         gather_words(3)
+        quantize_chunk(1)
+        gather_words(4)
         round_chunk(2)
         quantize_chunk(2)
-        gather_words(4)
-        round_chunk(3)
-        quantize_chunk(3)
 
         accs = {}
 
@@ -235,10 +233,10 @@ def tile_moe_two_lin_bias_kernel(tc, x_words, x_scales, w, b, gate, offs, dst, o
                     accs[e] = psum_acc.tile([P, C], F32, name="acc")
                 multiply(unit, accs[e])
 
-        multiply_units(0, first_unit[4])
-        for c in range(4, len(CHUNKS)):
+        multiply_units(0, first_unit[3])
+        for c in range(3, len(CHUNKS)):
             round_chunk(c)
-            due = [(e, gate_sums(e, accs[e])) for e in range(E - 1) if (load_first[FINISH_AFTER[e]] + LOADS[FINISH_AFTER[e]] - 1) // 2 == c]
+            due = [(e, gate_sums(e, accs[e])) for e in range(E - 1) if min(FINISH_AFTER[e], len(CHUNKS) - 1) == c]
             quantize_chunk(c)
             multiply_units(first_unit[c], first_unit[c] + CHUNKS[c])
             for e, gated in due:

@@ -23,7 +23,7 @@ PACK = 4
 PASSES = K // (P * PACK)
 UNITS = E * PASSES
 CHUNKS = [2, 4] + [2] * 17
-ON_VECTOR = (25, 37, 39)
+ON_VECTOR = (39,)
 BANK = 512
 ACC_BANKS = 5
 EARLY_PASSES = 1

@@ -23,13 +23,14 @@ PACK = 4
 PASSES = K // (P * PACK)
 UNITS = E * PASSES
 CHUNKS = [2, 4] + [2] * 17
-ON_VECTOR = (39,)
+ON_VECTOR = (18, 19, 20, 21, 28, 29, 30, 31, 34, 35, 38, 39)
 BANK = 512
 ACC_BANKS = 5
 EARLY_PASSES = 1
 EARLY_LOADS = 2
 LOADS = [2, 4] + [2] * 16 + [1, 1]
-FINISH_AFTER = (3, 5, 8, 9, 12, 14, 19)
+GROUPS = [(0, 1, 2), (3, 4), (5, 6)]
+FIRST_GROUP_HELD_BEHIND = 5
 
 
 def tile_moe_two_lin_bias_kernel(tc, x_words, x_scales, w, b, gate, offs, dst, out):
@@ -44,7 +45,7 @@ def tile_moe_two_lin_bias_kernel(tc, x_words, x_scales, w, b, gate, offs, dst, o
         dst_sb = keep.tile([P, SLOTS // 16], U16, name="dst_sb")
         ident = keep.tile([P, P], F32, name="ident")
         gate_sb = keep.tile([P, SLOTS], F32, name="gate_sb")
-        gated_bias = keep.tile([P, SLOTS], F32, name="gated_bias")
+        gated_bias = keep.tile([P, C], F32, name="gated_bias")
         out_sb = keep.tile([P, T], F32, name="out_sb")
         tok_words = [keep.tile([P, T], I32, name="tok_words%d" % a) for a in range(EARLY_PASSES)]
         slot_words = {a: keep.tile([P, SLOTS], U32, name="slot_words%d" % a, align_bytes=64) for a in range(PASSES)}
@@ -115,9 +116,7 @@ def tile_moe_two_lin_bias_kernel(tc, x_words, x_scales, w, b, gate, offs, dst, o
                     out=gate_sb[:].rearrange("n (p j) -> n p j", p=P)[:, :, h * per_bank : (h + 1) * per_bank],
                     in_=spread[:].rearrange("n j p -> n p j"),
                 )
-            for e in range(E):
-                cols = slice(e * C, (e + 1) * C)
-                nc.scalar.activation(out=gated_bias[:, cols], in_=gate_sb[:, cols], func=COPY, scale=b_sb[:, e : e + 1])
+            nc.scalar.activation(out=gated_bias[:], in_=gate_sb[:, (E - 1) * C :], func=COPY, scale=b_sb[:, E - 1 : E])
 
         def gather_words(a):
             nc.vector.tensor_copy(slot_words[a][:], tok_words[a][:].bitcast(U32).indirect(offs_sb[:]))
@@ -136,6 +135,12 @@ def tile_moe_two_lin_bias_kernel(tc, x_words, x_scales, w, b, gate, offs, dst, o
             units = range(first_unit[c], first_unit[c] + CHUNKS[c])
             if not any(unit in ON_VECTOR for unit in units):
                 nc.scalar.copy(
+                    out=w_bf[c][:].rearrange("p u (g m) j -> p u g j m", m=4),
+                    in_=raw_units(c).rearrange("p u j (g m) -> p u g j m", m=4),
+                )
+                return
+            if all(unit in ON_VECTOR for unit in units) and load_of[units[0]] == load_of[units[-1]]:
+                nc.vector.tensor_copy(
                     out=w_bf[c][:].rearrange("p u (g m) j -> p u g j m", m=4),
                     in_=raw_units(c).rearrange("p u j (g m) -> p u g j m", m=4),
                 )
@@ -172,17 +177,20 @@ def tile_moe_two_lin_bias_kernel(tc, x_words, x_scales, w, b, gate, offs, dst, o
                 stop=(a == PASSES - 1),
             )
 
-        def gate_sums(e, acc):
-            if e < E - 1:
-                gated = late.tile([P, C], F32, name="gated%d" % e, offset=raw_at(FINISH_AFTER[e]))
-            else:
-                gated = keep.tile([P, C], F32, name="gated%d" % e)
-            nc.vector.tensor_tensor(out=gated[:], in0=acc[:], in1=gate_sb[:, e * C : (e + 1) * C], op=MULT)
-            return gated
+        def finish(e, acc, gated):
+            nc.vector.scalar_tensor_tensor(
+                out=gated, in0=acc[:], scalar=b_sb[:, e : e + 1], in1=gate_sb[:, e * C : (e + 1) * C], op0=ADD, op1=MULT
+            )
 
-        def scatter(e, gated):
-            places = dst_sb[:, e * C // 16 : (e + 1) * C // 16]
-            nc.vector.tensor_tensor(out_sb[:].indirect(places), gated[:], gated_bias[:, e * C : (e + 1) * C], ADD)
+        def scatter_group(group, gated):
+            places = dst_sb[:, group[0] * C // 16 : (group[-1] + 1) * C // 16]
+            nc.scalar.activation(out_sb[:].indirect(places), gated[:], COPY)
+
+        def finish_last(acc):
+            e = E - 1
+            gated = keep.tile([P, C], F32, name="gated_last")
+            nc.vector.tensor_tensor(out=gated[:], in0=acc[:], in1=gate_sb[:, e * C :], op=MULT)
+            nc.vector.tensor_tensor(out_sb[:].indirect(dst_sb[:, e * C // 16 :]), gated[:], gated_bias[:], ADD)
 
         nc.sync.dma_start(offs_sb[:], offs)
         load_tokens(0)
@@ -234,13 +242,31 @@ def tile_moe_two_lin_bias_kernel(tc, x_words, x_scales, w, b, gate, offs, dst, o
                 multiply(unit, accs[e])
 
         multiply_units(0, first_unit[3])
+        gated = {}
+        finished = 0
+        to_scatter = []
         for c in range(3, len(CHUNKS)):
             round_chunk(c)
-            due = [(e, gate_sums(e, accs[e])) for e in range(E - 1) if min(FINISH_AFTER[e], len(CHUNKS) - 1) == c]
+            for group in to_scatter:
+                scatter_group(group, gated[group])
+            to_scatter = []
             quantize_chunk(c)
-            multiply_units(first_unit[c], first_unit[c] + CHUNKS[c])
-            for e, gated in due:
-                scatter(e, gated)
-        scatter(E - 1, gate_sums(E - 1, accs[E - 1]))
+            done = first_unit[c] + CHUNKS[c]
+            multiply_units(first_unit[c], done)
+            while c >= FIRST_GROUP_HELD_BEHIND and finished < min(done // PASSES, E - 1):
+                group = [g for g in GROUPS if finished in g][0]
+                if group not in gated:
+                    if group == GROUPS[0]:
+                        gated[group] = late.tile(
+                            [P, len(group) * C], F32, name="gated%d" % group[0], offset=raw_at(FIRST_GROUP_HELD_BEHIND)
+                        )
+                    else:
+                        gated[group] = keep.tile([P, len(group) * C], F32, name="gated%d" % group[0])
+                i = finished - group[0]
+                finish(finished, accs[finished], gated[group][:, i * C : (i + 1) * C])
+                if finished == group[-1]:
+                    to_scatter.append(group)
+                finished = finished + 1
+        finish_last(accs[E - 1])
 
         nc.sync.dma_start(out=out, in_=out_sb[:])

@@ -23,14 +23,15 @@ PACK = 4
 PASSES = K // (P * PACK)
 UNITS = E * PASSES
 CHUNKS = [2, 4] + [2] * 17
-ON_VECTOR = (18, 19, 20, 21, 28, 29, 30, 31, 34, 35, 38, 39)
+ON_VECTOR = (20, 21, 22, 23, 30, 31, 32, 33, 39)
 BANK = 512
 ACC_BANKS = 5
 EARLY_PASSES = 1
 EARLY_LOADS = 2
 LOADS = [2, 4] + [2] * 16 + [1, 1]
-GROUPS = [(0, 1, 2), (3, 4), (5, 6)]
-FIRST_GROUP_HELD_BEHIND = 5
+GROUPS = {7: (0, 1, 2), 12: (3, 4)}
+SINGLES = {15: 5, 19: 6}
+FIRST_SINGLE = 5
 
 
 def tile_moe_two_lin_bias_kernel(tc, x_words, x_scales, w, b, gate, offs, dst, out):
@@ -45,7 +46,7 @@ def tile_moe_two_lin_bias_kernel(tc, x_words, x_scales, w, b, gate, offs, dst, o
         dst_sb = keep.tile([P, SLOTS // 16], U16, name="dst_sb")
         ident = keep.tile([P, P], F32, name="ident")
         gate_sb = keep.tile([P, SLOTS], F32, name="gate_sb")
-        gated_bias = keep.tile([P, C], F32, name="gated_bias")
+        gated_bias = keep.tile([P, SLOTS], F32, name="gated_bias")
         out_sb = keep.tile([P, T], F32, name="out_sb")
         tok_words = [keep.tile([P, T], I32, name="tok_words%d" % a) for a in range(EARLY_PASSES)]
         slot_words = {a: keep.tile([P, SLOTS], U32, name="slot_words%d" % a, align_bytes=64) for a in range(PASSES)}
@@ -116,7 +117,9 @@ def tile_moe_two_lin_bias_kernel(tc, x_words, x_scales, w, b, gate, offs, dst, o
                     out=gate_sb[:].rearrange("n (p j) -> n p j", p=P)[:, :, h * per_bank : (h + 1) * per_bank],
                     in_=spread[:].rearrange("n j p -> n p j"),
                 )
-            nc.scalar.activation(out=gated_bias[:], in_=gate_sb[:, (E - 1) * C :], func=COPY, scale=b_sb[:, E - 1 : E])
+            for e in range(FIRST_SINGLE, E):
+                cols = slice(e * C, (e + 1) * C)
+                nc.scalar.activation(out=gated_bias[:, cols], in_=gate_sb[:, cols], func=COPY, scale=b_sb[:, e : e + 1])
 
         def gather_words(a):
             nc.vector.tensor_copy(slot_words[a][:], tok_words[a][:].bitcast(U32).indirect(offs_sb[:]))
@@ -177,20 +180,34 @@ def tile_moe_two_lin_bias_kernel(tc, x_words, x_scales, w, b, gate, offs, dst, o
                 stop=(a == PASSES - 1),
             )
 
-        def finish(e, acc, gated):
-            nc.vector.scalar_tensor_tensor(
-                out=gated, in0=acc[:], scalar=b_sb[:, e : e + 1], in1=gate_sb[:, e * C : (e + 1) * C], op0=ADD, op1=MULT
-            )
+        def finish_group(group, held_behind):
+            gated = late.tile([P, len(group) * C], F32, name="gated%d" % group[0], offset=raw_at(held_behind))
+            for i, e in enumerate(group):
+                nc.vector.scalar_tensor_tensor(
+                    out=gated[:, i * C : (i + 1) * C],
+                    in0=accs[e][:],
+                    scalar=b_sb[:, e : e + 1],
+                    in1=gate_sb[:, e * C : (e + 1) * C],
+                    op0=ADD,
+                    op1=MULT,
+                )
+            return gated
 
         def scatter_group(group, gated):
             places = dst_sb[:, group[0] * C // 16 : (group[-1] + 1) * C // 16]
             nc.scalar.activation(out_sb[:].indirect(places), gated[:], COPY)
 
-        def finish_last(acc):
-            e = E - 1
-            gated = keep.tile([P, C], F32, name="gated_last")
-            nc.vector.tensor_tensor(out=gated[:], in0=acc[:], in1=gate_sb[:, e * C :], op=MULT)
-            nc.vector.tensor_tensor(out_sb[:].indirect(dst_sb[:, e * C // 16 :]), gated[:], gated_bias[:], ADD)
+        def gate_sums(e, acc, held_behind):
+            if e < E - 1:
+                gated = late.tile([P, C], F32, name="gated%d" % e, offset=raw_at(held_behind))
+            else:
+                gated = keep.tile([P, C], F32, name="gated%d" % e)
+            nc.vector.tensor_tensor(out=gated[:], in0=acc[:], in1=gate_sb[:, e * C : (e + 1) * C], op=MULT)
+            return gated
+
+        def scatter(e, gated):
+            places = dst_sb[:, e * C // 16 : (e + 1) * C // 16]
+            nc.vector.tensor_tensor(out_sb[:].indirect(places), gated[:], gated_bias[:, e * C : (e + 1) * C], ADD)
 
         nc.sync.dma_start(offs_sb[:], offs)
         load_tokens(0)
@@ -242,31 +259,19 @@ def tile_moe_two_lin_bias_kernel(tc, x_words, x_scales, w, b, gate, offs, dst, o
                 multiply(unit, accs[e])
 
         multiply_units(0, first_unit[3])
-        gated = {}
-        finished = 0
-        to_scatter = []
+        gated_groups = {}
+        last = len(CHUNKS) - 1
         for c in range(3, len(CHUNKS)):
             round_chunk(c)
-            for group in to_scatter:
-                scatter_group(group, gated[group])
-            to_scatter = []
+            if c - 1 in GROUPS:
+                scatter_group(GROUPS[c - 1], gated_groups[c - 1])
+            if c in GROUPS:
+                gated_groups[c] = finish_group(GROUPS[c], c)
+            due = [(e, gate_sums(e, accs[e], d)) for d, e in sorted(zip(SINGLES, [SINGLES[k] for k in SINGLES])) if min(d, last) == c]
             quantize_chunk(c)
-            done = first_unit[c] + CHUNKS[c]
-            multiply_units(first_unit[c], done)
-            while c >= FIRST_GROUP_HELD_BEHIND and finished < min(done // PASSES, E - 1):
-                group = [g for g in GROUPS if finished in g][0]
-                if group not in gated:
-                    if group == GROUPS[0]:
-                        gated[group] = late.tile(
-                            [P, len(group) * C], F32, name="gated%d" % group[0], offset=raw_at(FIRST_GROUP_HELD_BEHIND)
-                        )
-                    else:
-                        gated[group] = keep.tile([P, len(group) * C], F32, name="gated%d" % group[0])
-                i = finished - group[0]
-                finish(finished, accs[finished], gated[group][:, i * C : (i + 1) * C])
-                if finished == group[-1]:
-                    to_scatter.append(group)
-                finished = finished + 1
-        finish_last(accs[E - 1])
+            multiply_units(first_unit[c], first_unit[c] + CHUNKS[c])
+            for e, gated in due:
+                scatter(e, gated)
+        scatter(E - 1, gate_sums(E - 1, accs[E - 1], None))
 
         nc.sync.dma_start(out=out, in_=out_sb[:])

@@ -22,87 +22,111 @@ P = 128
 PACK = 4
 PASSES = K // (P * PACK)
 UNITS = E * PASSES
-CHUNKS = [2, 4] + [2] * 17
-ON_VECTOR = (20, 21, 22, 23, 30, 31, 32, 33, 39)
+SHARED_PASSES = 4
+LIST_ROWS = 16
 BANK = 512
-ACC_BANKS = 5
-EARLY_PASSES = 1
-EARLY_LOADS = 2
+RUN = 4
+DMA_ALIGN = 256
+
 LOADS = [2, 4] + [2] * 16 + [1, 1]
-GROUPS = {7: (0, 1, 2), 12: (3, 4)}
-SINGLES = {15: 5, 19: 6}
+CHUNKS = LOADS[:-2] + [2]
+EARLY_LOADS = 2
+EARLY_CHUNKS = 3
+EARLY_PASSES = 3
+ACC_BANKS = 5
+
+GROUPS = [(0, 1, 2), (3, 4)]
+CHUNKS_AHEAD = [2, 1]
 FIRST_SINGLE = 5
+LAST_RUNS_ON_SCALAR = 12
 
 
 def tile_moe_two_lin_bias_kernel(tc, x_words, x_scales, w, b, gate, offs, dst, out):
     nc = tc.nc
     with ExitStack() as ctx:
         keep = ctx.enter_context(tc.tile_pool(name="keep", bufs=1))
-        late = ctx.enter_context(tc.tile_pool(name="late", bufs=1))
+        staged = ctx.enter_context(tc.tile_pool(name="staged", bufs=1))
         psum = ctx.enter_context(tc.psum_pool(name="psum", bufs=1))
         psum_acc = ctx.enter_context(tc.psum_pool(name="psum_acc", bufs=ACC_BANKS))
 
-        offs_sb = keep.tile([P, SLOTS // 16], U16, name="offs_sb")
-        dst_sb = keep.tile([P, SLOTS // 16], U16, name="dst_sb")
+        offs_sb = keep.tile([P, SLOTS // LIST_ROWS], U16, name="offs_sb")
+        dst_sb = keep.tile([P, SLOTS // LIST_ROWS], U16, name="dst_sb")
         ident = keep.tile([P, P], F32, name="ident")
         gate_sb = keep.tile([P, SLOTS], F32, name="gate_sb")
-        gated_bias = keep.tile([P, SLOTS], F32, name="gated_bias")
-        out_sb = keep.tile([P, T], F32, name="out_sb")
-        tok_words = [keep.tile([P, T], I32, name="tok_words%d" % a) for a in range(EARLY_PASSES)]
-        slot_words = {a: keep.tile([P, SLOTS], U32, name="slot_words%d" % a, align_bytes=64) for a in range(PASSES)}
+        gated_bias = keep.tile([P, (E - FIRST_SINGLE) * C], F32, name="gated_bias")
+        out_sb = keep.tile([P, T], F32, name="out_sb", align_bytes=DMA_ALIGN)
+        tok_words = [keep.tile([P, T], I32, name="tok_words0", align_bytes=DMA_ALIGN)]
+        slot_words = [keep.tile([P, SLOTS], U32, name="slot_words%d" % a, align_bytes=64) for a in range(PASSES)]
         slot_scales = keep.tile([P, SLOTS], U8, name="slot_scales", align_bytes=64)
         slot_scales_last = keep.tile([P, SLOTS], U8, name="slot_scales_last", align_bytes=64)
-
-        first_unit = [sum(CHUNKS[:c]) for c in range(len(CHUNKS))]
         w_bf = [keep.tile([P, u, N, PACK], BF16, name="w_bf%d" % c, align_bytes=64) for c, u in enumerate(CHUNKS)]
         w_codes = [keep.tile([P, u, N], U32, name="w_codes%d" % c, align_bytes=64) for c, u in enumerate(CHUNKS)]
         w_scales = [keep.tile([P, u, N], U8, name="w_scales%d" % c, align_bytes=64) for c, u in enumerate(CHUNKS)]
         w_rows = w.rearrange("e k n -> (e k) n")
 
-        unit_bytes = PACK * N * 4
-        words_bytes = T * 4
+        chunk_first = [sum(CHUNKS[:c]) for c in range(len(CHUNKS))]
+        chunk_of = [c for c, u in enumerate(CHUNKS) for i in range(u)]
         load_first = [sum(LOADS[:d]) for d in range(len(LOADS))]
         load_of = [d for d, u in enumerate(LOADS) for i in range(u)]
-        b_at = 2 * words_bytes
-        gate_at = b_at + 64
-        w_at = gate_at + 64
-        second_at = w_at + load_first[EARLY_LOADS] * unit_bytes
-        last_words_at = w_at + UNITS * unit_bytes
-        words_at = [None, 0, words_bytes, last_words_at, last_words_at + words_bytes]
-        zero_room = late.tile([P, second_at // 4], F32, name="zero_room", offset=0)
-        scale_room = late.tile(
-            [P, last_words_at + 2 * words_bytes - second_at], U8, name="scale_room", offset=second_at, align_bytes=64
-        )
-        tok_scales = scale_room[:, 0:T]
+        last_chunk = len(CHUNKS) - 1
+        last_load = len(LOADS) - 1
 
-        nc.vector.memset(tok_scales.bitcast(I32), 0)
-        nc.vector.memset(zero_room[:, 0:P], 0.0)
-        nc.vector.memset(slot_scales_last[:].bitcast(I32), 0)
-        nc.vector.tensor_copy(out=out_sb[:, 0:P], in_=zero_room[:, 0:P])
-        nc.vector.memset(out_sb[:, P:T], 0.0)
-        make_identity(nc, ident[:])
+        def closing_chunk(e):
+            return chunk_of[(e + 1) * PASSES - 1]
+
+        vector_units = [load_first[last_load - 1] - 1]
+        for group, ahead in zip(GROUPS, CHUNKS_AHEAD):
+            first = closing_chunk(group[-1]) + ahead + 1
+            vector_units.extend(range(chunk_first[first], chunk_first[first + len(group)]))
+
+        unit_bytes = PACK * N * 4
+        words_bytes = T * 4
+        b_at = (EARLY_PASSES - 1) * words_bytes
+        gate_at = b_at + 64
+        w_at = b_at + DMA_ALIGN
+        later_at = w_at + load_first[EARLY_LOADS] * unit_bytes
+        later_words_at = w_at + UNITS * unit_bytes
+        staged_bytes = later_words_at + (PASSES - EARLY_PASSES) * words_bytes
+
+        def words_at(a):
+            return (a - 1) * words_bytes if a < EARLY_PASSES else later_words_at + (a - EARLY_PASSES) * words_bytes
 
         def raw_at(d):
             return w_at + load_first[d] * unit_bytes
 
-        def raw_units(c):
-            d = load_of[first_unit[c]]
-            i = first_unit[c] - load_first[d]
-            return w_raw[d][:, i : i + CHUNKS[c]]
+        zeros = staged.tile([P, later_at // 4], F32, name="zeros", offset=0)
+        scale_rows = staged.tile([P, staged_bytes - later_at], U8, name="scale_rows", offset=later_at, align_bytes=DMA_ALIGN)
+        tok_scales = scale_rows[:, 0:T]
 
-        def load_scales(q):
-            nc.sync.dma_start(
-                out=scale_room[32 * q : 32 * q + 16, 0:T].bitcast(I32),
-                in_=x_scales[0:4, 4 * q : 4 * q + 4, :].bitcast(I32),
-            )
+        nc.vector.memset(tok_scales.bitcast(I32), 0)
+        nc.vector.memset(zeros[:, 0:P], 0.0)
+        nc.vector.memset(slot_scales_last[:].bitcast(I32), 0)
+        nc.vector.tensor_copy(out=out_sb[:, 0:P], in_=zeros[:, 0:P])
+        nc.vector.memset(out_sb[:, P:T], 0.0)
+        make_identity(nc, ident[:])
 
         def load_tokens(a):
             nc.sync.dma_start(out=tok_words[a][:], in_=x_words[a].rearrange("p t r -> p (t r)").bitcast(I32))
 
-        def load_w(c):
-            rows = w_rows[load_first[c] * P * PACK : (load_first[c] + LOADS[c]) * P * PACK, :]
+        def load_scales():
+            for q in range(4):
+                nc.sync.dma_start(
+                    out=scale_rows[32 * q : 32 * q + 16, 0:T].bitcast(I32),
+                    in_=x_scales[0:SHARED_PASSES, 4 * q : 4 * q + 4, :].bitcast(I32),
+                )
+            nc.sync.dma_start(out=scale_rows[16:32, 0:T].bitcast(I32), in_=x_scales[PASSES - 1].bitcast(I32))
+
+        def move_last_scales():
+            for q in range(4):
+                nc.sync.dma_start(
+                    out=slot_scales_last[32 * q : 32 * q + 4, :].bitcast(I32),
+                    in_=slot_scales[16 + 4 * q : 20 + 4 * q, :].bitcast(I32),
+                )
+
+        def load_w(d):
+            rows = w_rows[load_first[d] * P * PACK : (load_first[d] + LOADS[d]) * P * PACK, :]
             nc.sync.dma_start(
-                out=w_raw[c][:].rearrange("p u j n -> p u (j n)"),
+                out=w_raw[d][:].rearrange("p u j n -> p u (j n)"),
                 in_=rows.rearrange("(u p j) n -> p u (j n)", p=P, j=PACK),
             )
 
@@ -118,44 +142,42 @@ def tile_moe_two_lin_bias_kernel(tc, x_words, x_scales, w, b, gate, offs, dst, o
                     in_=spread[:].rearrange("n j p -> n p j"),
                 )
             for e in range(FIRST_SINGLE, E):
-                cols = slice(e * C, (e + 1) * C)
-                nc.scalar.activation(out=gated_bias[:, cols], in_=gate_sb[:, cols], func=COPY, scale=b_sb[:, e : e + 1])
+                nc.scalar.activation(out=single_bias(e), in_=gate_sb[:, slots(e)], func=COPY, scale=b_sb[:, e : e + 1])
+
+        def slots(e):
+            return slice(e * C, (e + 1) * C)
+
+        def single_bias(e):
+            return gated_bias[:, slots(e - FIRST_SINGLE)]
+
+        def places(first_expert, last_expert):
+            return dst_sb[:, first_expert * C // LIST_ROWS : (last_expert + 1) * C // LIST_ROWS]
 
         def gather_words(a):
             nc.vector.tensor_copy(slot_words[a][:], tok_words[a][:].bitcast(U32).indirect(offs_sb[:]))
 
-        def gather_scales():
-            nc.vector.tensor_copy(slot_scales[:], tok_scales.indirect(offs_sb[:]))
-
-        def move_last_scales():
-            for q in range(4):
-                nc.sync.dma_start(
-                    out=slot_scales_last[32 * q : 32 * q + 4, :].bitcast(I32),
-                    in_=slot_scales[16 + 4 * q : 20 + 4 * q, :].bitcast(I32),
-                )
-
         def round_chunk(c):
-            units = range(first_unit[c], first_unit[c] + CHUNKS[c])
-            if not any(unit in ON_VECTOR for unit in units):
-                nc.scalar.copy(
-                    out=w_bf[c][:].rearrange("p u (g m) j -> p u g j m", m=4),
-                    in_=raw_units(c).rearrange("p u j (g m) -> p u g j m", m=4),
-                )
-                return
-            if all(unit in ON_VECTOR for unit in units) and load_of[units[0]] == load_of[units[-1]]:
-                nc.vector.tensor_copy(
-                    out=w_bf[c][:].rearrange("p u (g m) j -> p u g j m", m=4),
-                    in_=raw_units(c).rearrange("p u j (g m) -> p u g j m", m=4),
-                )
+            units = range(chunk_first[c], chunk_first[c] + CHUNKS[c])
+            on_vector = [unit in vector_units for unit in units]
+            if c < last_chunk and all(v == on_vector[0] for v in on_vector):
+                rounded = w_bf[c][:].rearrange("p u (g m) j -> p u g j m", m=RUN)
+                raw = w_raw[c][:].rearrange("p u j (g m) -> p u g j m", m=RUN)
+                if on_vector[0]:
+                    nc.vector.tensor_copy(out=rounded, in_=raw)
+                else:
+                    nc.scalar.copy(out=rounded, in_=raw)
                 return
             for i, unit in enumerate(units):
                 d = load_of[unit]
-                src = w_raw[d][:, unit - load_first[d]].rearrange("p j (g m) -> p g j m", m=4)
-                tgt = w_bf[c][:, i].rearrange("p (g m) j -> p g j m", m=4)
-                if unit in ON_VECTOR:
-                    nc.vector.tensor_copy(out=tgt, in_=src)
+                rounded = w_bf[c][:, i].rearrange("p (g m) j -> p g j m", m=RUN)
+                raw = w_raw[d][:, unit - load_first[d]].rearrange("p j (g m) -> p g j m", m=RUN)
+                if d == last_load:
+                    nc.scalar.copy(out=rounded[:, :LAST_RUNS_ON_SCALAR], in_=raw[:, :LAST_RUNS_ON_SCALAR])
+                    nc.vector.tensor_copy(out=rounded[:, LAST_RUNS_ON_SCALAR:], in_=raw[:, LAST_RUNS_ON_SCALAR:])
+                elif on_vector[i]:
+                    nc.vector.tensor_copy(out=rounded, in_=raw)
                 else:
-                    nc.scalar.copy(out=tgt, in_=src)
+                    nc.scalar.copy(out=rounded, in_=raw)
 
         def quantize_chunk(c):
             nc.vector.quantize_mx(
@@ -164,63 +186,52 @@ def tile_moe_two_lin_bias_kernel(tc, x_words, x_scales, w, b, gate, offs, dst, o
                 in_=w_bf[c][:].rearrange("p u n j -> p (u n j)"),
             )
 
-        def multiply(unit, acc):
-            e, a = divmod(unit, PASSES)
-            c = max(cc for cc in range(len(CHUNKS)) if first_unit[cc] <= unit)
-            i = unit - first_unit[c]
-            cols = slice(e * C, (e + 1) * C)
-            rhs_scale = slot_scales[4 * a :, cols] if a < 4 else slot_scales_last[:, cols]
-            nc.tensor.matmul_mx(
-                out=acc[:],
-                lhsT=w_codes[c][:, i, :].bitcast(FP8X4),
-                lhsT_scale=w_scales[c][:, i, :],
-                rhs=slot_words[a][:, cols].bitcast(FP8X4),
-                rhs_scale=rhs_scale,
-                start=(a == 0),
-                stop=(a == PASSES - 1),
-            )
+        sums = {}
 
-        def finish_group(group, held_behind):
-            gated = late.tile([P, len(group) * C], F32, name="gated%d" % group[0], offset=raw_at(held_behind))
+        def multiply_chunk(c):
+            for i in range(CHUNKS[c]):
+                e, a = divmod(chunk_first[c] + i, PASSES)
+                if a == 0:
+                    sums[e] = psum_acc.tile([P, C], F32, name="sums")
+                nc.tensor.matmul_mx(
+                    out=sums[e][:],
+                    lhsT=w_codes[c][:, i, :].bitcast(FP8X4),
+                    lhsT_scale=w_scales[c][:, i, :],
+                    rhs=slot_words[a][:, slots(e)].bitcast(FP8X4),
+                    rhs_scale=slot_scales[4 * a :, slots(e)] if a < SHARED_PASSES else slot_scales_last[:, slots(e)],
+                    start=(a == 0),
+                    stop=(a == PASSES - 1),
+                )
+
+        def gate_group(group, behind_load):
+            gated = staged.tile([P, len(group) * C], F32, name="gated%d" % group[0], offset=raw_at(behind_load))
             for i, e in enumerate(group):
                 nc.vector.scalar_tensor_tensor(
-                    out=gated[:, i * C : (i + 1) * C],
-                    in0=accs[e][:],
+                    out=gated[:, slots(i)],
+                    in0=sums[e][:],
                     scalar=b_sb[:, e : e + 1],
-                    in1=gate_sb[:, e * C : (e + 1) * C],
+                    in1=gate_sb[:, slots(e)],
                     op0=ADD,
                     op1=MULT,
                 )
             return gated
 
-        def scatter_group(group, gated):
-            places = dst_sb[:, group[0] * C // 16 : (group[-1] + 1) * C // 16]
-            nc.scalar.activation(out_sb[:].indirect(places), gated[:], COPY)
+        def gate_single(e, gated):
+            nc.vector.tensor_tensor(out=gated[:], in0=sums[e][:], in1=gate_sb[:, slots(e)], op=MULT)
 
-        def gate_sums(e, acc, held_behind):
-            if e < E - 1:
-                gated = late.tile([P, C], F32, name="gated%d" % e, offset=raw_at(held_behind))
-            else:
-                gated = keep.tile([P, C], F32, name="gated%d" % e)
-            nc.vector.tensor_tensor(out=gated[:], in0=acc[:], in1=gate_sb[:, e * C : (e + 1) * C], op=MULT)
-            return gated
-
-        def scatter(e, gated):
-            places = dst_sb[:, e * C // 16 : (e + 1) * C // 16]
-            nc.vector.tensor_tensor(out_sb[:].indirect(places), gated[:], gated_bias[:, e * C : (e + 1) * C], ADD)
+        def scatter_single(e, gated):
+            nc.vector.tensor_tensor(out_sb[:].indirect(places(e, e)), gated[:], single_bias(e), ADD)
 
         nc.sync.dma_start(offs_sb[:], offs)
         load_tokens(0)
         nc.sync.dma_start(dst_sb[:], dst)
-        for q in range(4):
-            load_scales(q)
-        nc.sync.dma_start(out=scale_room[16:32, 0:T].bitcast(I32), in_=x_scales[PASSES - 1].bitcast(I32))
+        load_scales()
 
-        for a in range(EARLY_PASSES, 3):
-            tok_words.append(late.tile([P, T], I32, name="tok_words%d" % a, offset=words_at[a]))
-        b_sb = late.tile([P, E], F32, name="b_sb", offset=b_at)
-        gate_cols = late.tile([P, SLOTS // P], F32, name="gate_cols", offset=gate_at)
-        w_raw = [late.tile([P, u, PACK, N], F32, name="w_raw%d" % d, offset=raw_at(d)) for d, u in enumerate(LOADS[:EARLY_LOADS])]
+        for a in range(1, EARLY_PASSES):
+            tok_words.append(staged.tile([P, T], I32, name="tok_words%d" % a, offset=words_at(a)))
+        b_sb = staged.tile([P, E], F32, name="b_sb", offset=b_at)
+        gate_cols = staged.tile([P, SLOTS // P], F32, name="gate_cols", offset=gate_at)
+        w_raw = [staged.tile([P, LOADS[d], PACK, N], F32, name="w_raw%d" % d, offset=raw_at(d)) for d in range(EARLY_LOADS)]
         load_tokens(1)
         load_w(0)
         nc.sync.dma_start(out=gate_cols[:], in_=gate[0, :].rearrange("(p j) -> p j", p=P))
@@ -229,14 +240,15 @@ def tile_moe_two_lin_bias_kernel(tc, x_words, x_scales, w, b, gate, offs, dst, o
         load_w(1)
 
         gather_words(0)
-        gather_scales()
+        nc.vector.tensor_copy(slot_scales[:], tok_scales.indirect(offs_sb[:]))
         move_last_scales()
-        for a in range(3, PASSES):
-            tok_words.append(late.tile([P, T], I32, name="tok_words%d" % a, offset=words_at[a]))
+        for a in range(EARLY_PASSES, PASSES):
+            tok_words.append(staged.tile([P, T], I32, name="tok_words%d" % a, offset=words_at(a)))
             load_tokens(a)
         for d in range(EARLY_LOADS, len(LOADS)):
-            w_raw.append(late.tile([P, LOADS[d], PACK, N], F32, name="w_raw%d" % d, offset=raw_at(d)))
+            w_raw.append(staged.tile([P, LOADS[d], PACK, N], F32, name="w_raw%d" % d, offset=raw_at(d)))
             load_w(d)
+
         gather_words(1)
         spread_gate()
         round_chunk(0)
@@ -248,30 +260,30 @@ def tile_moe_two_lin_bias_kernel(tc, x_words, x_scales, w, b, gate, offs, dst, o
         gather_words(4)
         round_chunk(2)
         quantize_chunk(2)
+        for c in range(EARLY_CHUNKS):
+            multiply_chunk(c)
 
-        accs = {}
-
-        def multiply_units(u0, u1):
-            for unit in range(u0, u1):
-                e = unit // PASSES
-                if e not in accs:
-                    accs[e] = psum_acc.tile([P, C], F32, name="acc")
-                multiply(unit, accs[e])
-
-        multiply_units(0, first_unit[3])
+        single_behind = {closing_chunk(FIRST_SINGLE) + 1: FIRST_SINGLE, last_chunk: E - 2}
         gated_groups = {}
-        last = len(CHUNKS) - 1
-        for c in range(3, len(CHUNKS)):
+        for c in range(EARLY_CHUNKS, len(CHUNKS)):
             round_chunk(c)
-            if c - 1 in GROUPS:
-                scatter_group(GROUPS[c - 1], gated_groups[c - 1])
-            if c in GROUPS:
-                gated_groups[c] = finish_group(GROUPS[c], c)
-            due = [(e, gate_sums(e, accs[e], d)) for d, e in sorted(zip(SINGLES, [SINGLES[k] for k in SINGLES])) if min(d, last) == c]
+            for group, ahead in zip(GROUPS, CHUNKS_AHEAD):
+                closing = closing_chunk(group[-1])
+                if c == closing + 1:
+                    gated_groups[group] = gate_group(group, closing + ahead - 1)
+                if c == closing + 2:
+                    nc.scalar.activation(out_sb[:].indirect(places(group[0], group[-1])), gated_groups[group][:], COPY)
+            single = single_behind.get(c)
+            if single is not None:
+                behind_load = load_of[chunk_first[c] + CHUNKS[c] - 1]
+                gated_single = staged.tile([P, C], F32, name="gated%d" % single, offset=raw_at(behind_load))
+                gate_single(single, gated_single)
             quantize_chunk(c)
-            multiply_units(first_unit[c], first_unit[c] + CHUNKS[c])
-            for e, gated in due:
-                scatter(e, gated)
-        scatter(E - 1, gate_sums(E - 1, accs[E - 1], None))
+            multiply_chunk(c)
+            if single is not None:
+                scatter_single(single, gated_single)
+        gated_last = keep.tile([P, C], F32, name="gated_last")
+        gate_single(E - 1, gated_last)
+        scatter_single(E - 1, gated_last)
 
         nc.sync.dma_start(out=out, in_=out_sb[:])

@@ -109,18 +109,18 @@ def tile_moe_two_lin_bias_kernel(tc, x_words, x_scales, w, b, gate, offs, dst, o
             nc.sync.dma_start(out=tok_words[a][:], in_=x_words[a].rearrange("p t r -> p (t r)").bitcast(I32))
 
         def load_scales():
-            for q in range(4):
+            nc.sync.dma_start(out=scale_rows[16:32, 0:T].bitcast(I32), in_=x_scales[PASSES - 1].bitcast(I32))
+            for q in (2, 3, 0, 1):
                 nc.sync.dma_start(
                     out=scale_rows[32 * q : 32 * q + 16, 0:T].bitcast(I32),
                     in_=x_scales[0:SHARED_PASSES, 4 * q : 4 * q + 4, :].bitcast(I32),
                 )
-            nc.sync.dma_start(out=scale_rows[16:32, 0:T].bitcast(I32), in_=x_scales[PASSES - 1].bitcast(I32))
 
         def move_last_scales():
-            for q in range(4):
+            for r in range(4):
                 nc.sync.dma_start(
-                    out=slot_scales_last[32 * q : 32 * q + 4, :].bitcast(I32),
-                    in_=slot_scales[16 + 4 * q : 20 + 4 * q, :].bitcast(I32),
+                    out=slot_scales_last[r:P:32, :].bitcast(I32),
+                    in_=slot_scales[16 + r : 32 : 4, :].bitcast(I32),
                 )
 
         def load_w(d):

@@ -28,17 +28,18 @@ BANK = 512
 RUN = 4
 DMA_ALIGN = 256
 
-LOADS = [2, 4] + [2] * 16 + [1, 1]
-CHUNKS = LOADS[:-2] + [2]
-EARLY_LOADS = 2
-EARLY_CHUNKS = 3
-EARLY_PASSES = 3
+HALF = C // 2
+
+CHUNKS = [2, 4] + [2] * 14 + [1, 2, 1, 1, 1]
+CHUNKS_AHEAD_OF_MOVES = 2
+PASSES_AHEAD_OF_MOVES = 3
+CHUNKS_AMONG_GATHERS = 3
 ACC_BANKS = 5
 
 GROUPS = [(0, 1, 2), (3, 4)]
 CHUNKS_AHEAD = [2, 1]
-FIRST_SINGLE = 5
-LAST_RUNS_ON_SCALAR = 12
+SPLIT_EXPERT = 5
+VECTOR_SLOTS = {SPLIT_EXPERT: HALF, E - 1: C}
 
 
 def tile_moe_two_lin_bias_kernel(tc, x_words, x_scales, w, b, gate, offs, dst, out):
@@ -53,7 +54,7 @@ def tile_moe_two_lin_bias_kernel(tc, x_words, x_scales, w, b, gate, offs, dst, o
         dst_sb = keep.tile([P, SLOTS // LIST_ROWS], U16, name="dst_sb")
         ident = keep.tile([P, P], F32, name="ident")
         gate_sb = keep.tile([P, SLOTS], F32, name="gate_sb")
-        gated_bias = keep.tile([P, (E - FIRST_SINGLE) * C], F32, name="gated_bias")
+        gated_bias = keep.tile([P, HALF + C], F32, name="gated_bias")
         out_sb = keep.tile([P, T], F32, name="out_sb", align_bytes=DMA_ALIGN)
         tok_words = [keep.tile([P, T], I32, name="tok_words0", align_bytes=DMA_ALIGN)]
         slot_words = [keep.tile([P, SLOTS], U32, name="slot_words%d" % a, align_bytes=64) for a in range(PASSES)]
@@ -66,33 +67,35 @@ def tile_moe_two_lin_bias_kernel(tc, x_words, x_scales, w, b, gate, offs, dst, o
 
         chunk_first = [sum(CHUNKS[:c]) for c in range(len(CHUNKS))]
         chunk_of = [c for c, u in enumerate(CHUNKS) for i in range(u)]
-        load_first = [sum(LOADS[:d]) for d in range(len(LOADS))]
-        load_of = [d for d, u in enumerate(LOADS) for i in range(u)]
         last_chunk = len(CHUNKS) - 1
-        last_load = len(LOADS) - 1
 
         def closing_chunk(e):
             return chunk_of[(e + 1) * PASSES - 1]
 
-        vector_units = [load_first[last_load - 1] - 1]
+        vector_chunks = [closing_chunk(E - 2), last_chunk - 2, last_chunk]
         for group, ahead in zip(GROUPS, CHUNKS_AHEAD):
             first = closing_chunk(group[-1]) + ahead + 1
-            vector_units.extend(range(chunk_first[first], chunk_first[first + len(group)]))
+            vector_chunks.extend(range(first, first + len(group)))
 
         unit_bytes = PACK * N * 4
         words_bytes = T * 4
-        b_at = (EARLY_PASSES - 1) * words_bytes
+        b_at = (PASSES_AHEAD_OF_MOVES - 1) * words_bytes
         gate_at = b_at + 64
         w_at = b_at + DMA_ALIGN
-        later_at = w_at + load_first[EARLY_LOADS] * unit_bytes
+        later_at = w_at + chunk_first[CHUNKS_AHEAD_OF_MOVES] * unit_bytes
         later_words_at = w_at + UNITS * unit_bytes
-        staged_bytes = later_words_at + (PASSES - EARLY_PASSES) * words_bytes
+        staged_bytes = later_words_at + (PASSES - PASSES_AHEAD_OF_MOVES) * words_bytes
 
         def words_at(a):
-            return (a - 1) * words_bytes if a < EARLY_PASSES else later_words_at + (a - EARLY_PASSES) * words_bytes
+            if a < PASSES_AHEAD_OF_MOVES:
+                return (a - 1) * words_bytes
+            return later_words_at + (a - PASSES_AHEAD_OF_MOVES) * words_bytes
 
-        def raw_at(d):
-            return w_at + load_first[d] * unit_bytes
+        def raw_at(c):
+            return w_at + chunk_first[c] * unit_bytes
+
+        def raw_tile(c):
+            return staged.tile([P, CHUNKS[c], PACK, N], F32, name="w_raw%d" % c, offset=raw_at(c))
 
         zeros = staged.tile([P, later_at // 4], F32, name="zeros", offset=0)
         scale_rows = staged.tile([P, staged_bytes - later_at], U8, name="scale_rows", offset=later_at, align_bytes=DMA_ALIGN)
@@ -123,10 +126,10 @@ def tile_moe_two_lin_bias_kernel(tc, x_words, x_scales, w, b, gate, offs, dst, o
                     in_=slot_scales[16 + r : 32 : 4, :].bitcast(I32),
                 )
 
-        def load_w(d):
-            rows = w_rows[load_first[d] * P * PACK : (load_first[d] + LOADS[d]) * P * PACK, :]
+        def load_w(c):
+            rows = w_rows[chunk_first[c] * P * PACK : (chunk_first[c] + CHUNKS[c]) * P * PACK, :]
             nc.sync.dma_start(
-                out=w_raw[d][:].rearrange("p u j n -> p u (j n)"),
+                out=w_raw[c][:].rearrange("p u j n -> p u (j n)"),
                 in_=rows.rearrange("(u p j) n -> p u (j n)", p=P, j=PACK),
             )
 
@@ -141,43 +144,31 @@ def tile_moe_two_lin_bias_kernel(tc, x_words, x_scales, w, b, gate, offs, dst, o
                     out=gate_sb[:].rearrange("n (p j) -> n p j", p=P)[:, :, h * per_bank : (h + 1) * per_bank],
                     in_=spread[:].rearrange("n j p -> n p j"),
                 )
-            for e in range(FIRST_SINGLE, E):
-                nc.scalar.activation(out=single_bias(e), in_=gate_sb[:, slots(e)], func=COPY, scale=b_sb[:, e : e + 1])
+            for e in VECTOR_SLOTS:
+                nc.scalar.activation(out=bias_of(e), in_=gate_sb[:, vector_slots(e)], func=COPY, scale=b_sb[:, e : e + 1])
 
         def slots(e):
             return slice(e * C, (e + 1) * C)
 
-        def single_bias(e):
-            return gated_bias[:, slots(e - FIRST_SINGLE)]
+        def vector_slots(e):
+            return slice(e * C, e * C + VECTOR_SLOTS[e])
 
-        def places(first_expert, last_expert):
-            return dst_sb[:, first_expert * C // LIST_ROWS : (last_expert + 1) * C // LIST_ROWS]
+        def bias_of(e):
+            return gated_bias[:, 0:HALF] if e == SPLIT_EXPERT else gated_bias[:, HALF:]
+
+        def places(first_slot, count):
+            return dst_sb[:, first_slot // LIST_ROWS : (first_slot + count) // LIST_ROWS]
 
         def gather_words(a):
             nc.vector.tensor_copy(slot_words[a][:], tok_words[a][:].bitcast(U32).indirect(offs_sb[:]))
 
         def round_chunk(c):
-            units = range(chunk_first[c], chunk_first[c] + CHUNKS[c])
-            on_vector = [unit in vector_units for unit in units]
-            if c < last_chunk and all(v == on_vector[0] for v in on_vector):
-                rounded = w_bf[c][:].rearrange("p u (g m) j -> p u g j m", m=RUN)
-                raw = w_raw[c][:].rearrange("p u j (g m) -> p u g j m", m=RUN)
-                if on_vector[0]:
-                    nc.vector.tensor_copy(out=rounded, in_=raw)
-                else:
-                    nc.scalar.copy(out=rounded, in_=raw)
-                return
-            for i, unit in enumerate(units):
-                d = load_of[unit]
-                rounded = w_bf[c][:, i].rearrange("p (g m) j -> p g j m", m=RUN)
-                raw = w_raw[d][:, unit - load_first[d]].rearrange("p j (g m) -> p g j m", m=RUN)
-                if d == last_load:
-                    nc.scalar.copy(out=rounded[:, :LAST_RUNS_ON_SCALAR], in_=raw[:, :LAST_RUNS_ON_SCALAR])
-                    nc.vector.tensor_copy(out=rounded[:, LAST_RUNS_ON_SCALAR:], in_=raw[:, LAST_RUNS_ON_SCALAR:])
-                elif on_vector[i]:
-                    nc.vector.tensor_copy(out=rounded, in_=raw)
-                else:
-                    nc.scalar.copy(out=rounded, in_=raw)
+            rounded = w_bf[c][:].rearrange("p u (g m) j -> p u g j m", m=RUN)
+            raw = w_raw[c][:].rearrange("p u j (g m) -> p u g j m", m=RUN)
+            if c in vector_chunks:
+                nc.vector.tensor_copy(out=rounded, in_=raw)
+            else:
+                nc.scalar.copy(out=rounded, in_=raw)
 
         def quantize_chunk(c):
             nc.vector.quantize_mx(
@@ -203,35 +194,37 @@ def tile_moe_two_lin_bias_kernel(tc, x_words, x_scales, w, b, gate, offs, dst, o
                     stop=(a == PASSES - 1),
                 )
 
-        def gate_group(group, behind_load):
-            gated = staged.tile([P, len(group) * C], F32, name="gated%d" % group[0], offset=raw_at(behind_load))
-            for i, e in enumerate(group):
-                nc.vector.scalar_tensor_tensor(
-                    out=gated[:, slots(i)],
-                    in0=sums[e][:],
-                    scalar=b_sb[:, e : e + 1],
-                    in1=gate_sb[:, slots(e)],
-                    op0=ADD,
-                    op1=MULT,
-                )
-            return gated
+        def add_bias_and_gate(gated, e, first):
+            nc.vector.scalar_tensor_tensor(
+                out=gated,
+                in0=sums[e][:, first:C],
+                scalar=b_sb[:, e : e + 1],
+                in1=gate_sb[:, e * C + first : (e + 1) * C],
+                op0=ADD,
+                op1=MULT,
+            )
 
-        def gate_single(e, gated):
-            nc.vector.tensor_tensor(out=gated[:], in0=sums[e][:], in1=gate_sb[:, slots(e)], op=MULT)
+        def scatter_on_scalar(first_slot, count, gated):
+            nc.scalar.activation(out_sb[:].indirect(places(first_slot, count)), gated[:], COPY)
 
-        def scatter_single(e, gated):
-            nc.vector.tensor_tensor(out_sb[:].indirect(places(e, e)), gated[:], single_bias(e), ADD)
+        def gate_alone(e, gated):
+            nc.vector.tensor_tensor(
+                out=gated[:], in0=sums[e][:, 0 : VECTOR_SLOTS[e]], in1=gate_sb[:, vector_slots(e)], op=MULT
+            )
+
+        def scatter_on_vector(e, gated):
+            nc.vector.tensor_tensor(out_sb[:].indirect(places(e * C, VECTOR_SLOTS[e])), gated[:], bias_of(e), ADD)
 
         nc.sync.dma_start(offs_sb[:], offs)
         load_tokens(0)
         nc.sync.dma_start(dst_sb[:], dst)
         load_scales()
 
-        for a in range(1, EARLY_PASSES):
+        for a in range(1, PASSES_AHEAD_OF_MOVES):
             tok_words.append(staged.tile([P, T], I32, name="tok_words%d" % a, offset=words_at(a)))
         b_sb = staged.tile([P, E], F32, name="b_sb", offset=b_at)
         gate_cols = staged.tile([P, SLOTS // P], F32, name="gate_cols", offset=gate_at)
-        w_raw = [staged.tile([P, LOADS[d], PACK, N], F32, name="w_raw%d" % d, offset=raw_at(d)) for d in range(EARLY_LOADS)]
+        w_raw = [raw_tile(c) for c in range(CHUNKS_AHEAD_OF_MOVES)]
         load_tokens(1)
         load_w(0)
         nc.sync.dma_start(out=gate_cols[:], in_=gate[0, :].rearrange("(p j) -> p j", p=P))
@@ -242,12 +235,12 @@ def tile_moe_two_lin_bias_kernel(tc, x_words, x_scales, w, b, gate, offs, dst, o
         gather_words(0)
         nc.vector.tensor_copy(slot_scales[:], tok_scales.indirect(offs_sb[:]))
         move_last_scales()
-        for a in range(EARLY_PASSES, PASSES):
+        for a in range(PASSES_AHEAD_OF_MOVES, PASSES):
             tok_words.append(staged.tile([P, T], I32, name="tok_words%d" % a, offset=words_at(a)))
             load_tokens(a)
-        for d in range(EARLY_LOADS, len(LOADS)):
-            w_raw.append(staged.tile([P, LOADS[d], PACK, N], F32, name="w_raw%d" % d, offset=raw_at(d)))
-            load_w(d)
+        for c in range(CHUNKS_AHEAD_OF_MOVES, len(CHUNKS)):
+            w_raw.append(raw_tile(c))
+            load_w(c)
 
         gather_words(1)
         spread_gate()
@@ -260,30 +253,37 @@ def tile_moe_two_lin_bias_kernel(tc, x_words, x_scales, w, b, gate, offs, dst, o
         gather_words(4)
         round_chunk(2)
         quantize_chunk(2)
-        for c in range(EARLY_CHUNKS):
+        for c in range(CHUNKS_AMONG_GATHERS):
             multiply_chunk(c)
 
-        single_behind = {closing_chunk(FIRST_SINGLE) + 1: FIRST_SINGLE, last_chunk: E - 2}
         gated_groups = {}
-        for c in range(EARLY_CHUNKS, len(CHUNKS)):
+        for c in range(CHUNKS_AMONG_GATHERS, len(CHUNKS)):
             round_chunk(c)
             for group, ahead in zip(GROUPS, CHUNKS_AHEAD):
                 closing = closing_chunk(group[-1])
                 if c == closing + 1:
-                    gated_groups[group] = gate_group(group, closing + ahead - 1)
+                    at = raw_at(closing + ahead - 1)
+                    gated_groups[group] = staged.tile([P, len(group) * C], F32, name="gated%d" % group[0], offset=at)
+                    for i, e in enumerate(group):
+                        add_bias_and_gate(gated_groups[group][:, slots(i)], e, 0)
                 if c == closing + 2:
-                    nc.scalar.activation(out_sb[:].indirect(places(group[0], group[-1])), gated_groups[group][:], COPY)
-            single = single_behind.get(c)
-            if single is not None:
-                behind_load = load_of[chunk_first[c] + CHUNKS[c] - 1]
-                gated_single = staged.tile([P, C], F32, name="gated%d" % single, offset=raw_at(behind_load))
-                gate_single(single, gated_single)
+                    scatter_on_scalar(group[0] * C, len(group) * C, gated_groups[group])
+            if c == closing_chunk(E - 2) + 1:
+                gated_rest = staged.tile([P, HALF + C], F32, name="gated_rest", offset=raw_at(c))
+                add_bias_and_gate(gated_rest[:, 0:HALF], SPLIT_EXPERT, HALF)
+                add_bias_and_gate(gated_rest[:, HALF:], E - 2, 0)
+            behind_split_expert = c == closing_chunk(SPLIT_EXPERT) + 1
+            if behind_split_expert:
+                gated_half = staged.tile([P, HALF], F32, name="gated_half", offset=raw_at(c))
+                gate_alone(SPLIT_EXPERT, gated_half)
             quantize_chunk(c)
             multiply_chunk(c)
-            if single is not None:
-                scatter_single(single, gated_single)
+            if c == last_chunk - 1:
+                scatter_on_scalar(SPLIT_EXPERT * C + HALF, HALF + C, gated_rest)
+            if behind_split_expert:
+                scatter_on_vector(SPLIT_EXPERT, gated_half)
         gated_last = keep.tile([P, C], F32, name="gated_last")
-        gate_single(E - 1, gated_last)
-        scatter_single(E - 1, gated_last)
+        gate_alone(E - 1, gated_last)
+        scatter_on_vector(E - 1, gated_last)
 
         nc.sync.dma_start(out=out, in_=out_sb[:])

@@ -31,7 +31,7 @@ DMA_ALIGN = 256
 HALF = C // 2
 
 CHUNKS = [2, 4] + [2] * 14 + [1, 2, 1, 1, 1]
-CHUNKS_AHEAD_OF_MOVES = 2
+CHUNKS_AHEAD_OF_MOVES = 3
 PASSES_AHEAD_OF_MOVES = 3
 CHUNKS_AMONG_GATHERS = 3
 ACC_BANKS = 5
@@ -231,6 +231,7 @@ def tile_moe_two_lin_bias_kernel(tc, x_words, x_scales, w, b, gate, offs, dst, o
         nc.sync.dma_start(out=b_sb[:], in_=b)
         load_tokens(2)
         load_w(1)
+        load_w(2)
 
         gather_words(0)
         nc.vector.tensor_copy(slot_scales[:], tok_scales.indirect(offs_sb[:]))

@@ -30,10 +30,9 @@ DMA_ALIGN = 256
 
 HALF = C // 2
 
-CHUNKS = [2, 4] + [2] * 14 + [1, 2, 1, 1, 1]
-CHUNKS_AHEAD_OF_MOVES = 3
-PASSES_AHEAD_OF_MOVES = 3
-CHUNKS_AMONG_GATHERS = 3
+CHUNKS = [2] * 17 + [1, 2, 1, 1, 1]
+CHUNKS_AHEAD_OF_MOVES = 5
+CHUNKS_AMONG_GATHERS = 4
 ACC_BANKS = 5
 
 GROUPS = [(0, 1, 2), (3, 4)]
@@ -56,8 +55,10 @@ def tile_moe_two_lin_bias_kernel(tc, x_words, x_scales, w, b, gate, offs, dst, o
         gate_sb = keep.tile([P, SLOTS], F32, name="gate_sb")
         gated_bias = keep.tile([P, HALF + C], F32, name="gated_bias")
         out_sb = keep.tile([P, T], F32, name="out_sb", align_bytes=DMA_ALIGN)
-        tok_words = [keep.tile([P, T], I32, name="tok_words0", align_bytes=DMA_ALIGN)]
-        slot_words = [keep.tile([P, SLOTS], U32, name="slot_words%d" % a, align_bytes=64) for a in range(PASSES)]
+        tok_words = [keep.tile([P, T], I32, name="tok_words%d" % a, align_bytes=DMA_ALIGN) for a in range(PASSES)]
+        b_sb = keep.tile([P, E], F32, name="b_sb")
+        gate_cols = keep.tile([P, SLOTS // P], F32, name="gate_cols")
+        slot_words = {a: keep.tile([P, SLOTS], U32, name="slot_words%d" % a, align_bytes=64) for a in range(PASSES) if a != 3}
         slot_scales = keep.tile([P, SLOTS], U8, name="slot_scales", align_bytes=64)
         slot_scales_last = keep.tile([P, SLOTS], U8, name="slot_scales_last", align_bytes=64)
         w_bf = [keep.tile([P, u, N, PACK], BF16, name="w_bf%d" % c, align_bytes=64) for c, u in enumerate(CHUNKS)]
@@ -78,43 +79,30 @@ def tile_moe_two_lin_bias_kernel(tc, x_words, x_scales, w, b, gate, offs, dst, o
             vector_chunks.extend(range(first, first + len(group)))
 
         unit_bytes = PACK * N * 4
-        words_bytes = T * 4
-        b_at = (PASSES_AHEAD_OF_MOVES - 1) * words_bytes
-        gate_at = b_at + 64
-        w_at = b_at + DMA_ALIGN
-        later_at = w_at + chunk_first[CHUNKS_AHEAD_OF_MOVES] * unit_bytes
-        later_words_at = w_at + UNITS * unit_bytes
-        staged_bytes = later_words_at + (PASSES - PASSES_AHEAD_OF_MOVES) * words_bytes
-
-        def words_at(a):
-            if a < PASSES_AHEAD_OF_MOVES:
-                return (a - 1) * words_bytes
-            return later_words_at + (a - PASSES_AHEAD_OF_MOVES) * words_bytes
+        later_at = chunk_first[CHUNKS_AHEAD_OF_MOVES] * unit_bytes
+        held_words_at = UNITS * unit_bytes
+        staged_bytes = held_words_at + SLOTS * 4
 
         def raw_at(c):
-            return w_at + chunk_first[c] * unit_bytes
+            return chunk_first[c] * unit_bytes
 
         def raw_tile(c):
             return staged.tile([P, CHUNKS[c], PACK, N], F32, name="w_raw%d" % c, offset=raw_at(c))
 
-        zeros = staged.tile([P, later_at // 4], F32, name="zeros", offset=0)
         scale_rows = staged.tile([P, staged_bytes - later_at], U8, name="scale_rows", offset=later_at, align_bytes=DMA_ALIGN)
         tok_scales = scale_rows[:, 0:T]
 
         nc.vector.memset(tok_scales.bitcast(I32), 0)
-        nc.vector.memset(zeros[:, 0:P], 0.0)
         nc.vector.memset(slot_scales_last[:].bitcast(I32), 0)
-        nc.vector.tensor_copy(out=out_sb[:, 0:P], in_=zeros[:, 0:P])
-        nc.vector.memset(out_sb[:, P:T], 0.0)
+        nc.vector.memset(out_sb[:], 0.0)
         make_identity(nc, ident[:])
 
         def load_tokens(a):
             nc.sync.dma_start(out=tok_words[a][:], in_=x_words[a].rearrange("p t r -> p (t r)").bitcast(I32))
 
         def load_scales():
-            nc.sync.dma_start(out=scale_rows[16:32, 0:T].bitcast(I32), in_=x_scales[PASSES - 1].bitcast(I32))
-            for q in (2, 3, 0, 1):
-                nc.sync.dma_start(
+            for q in range(4):
+                nc.gpsimd.dma_start(
                     out=scale_rows[32 * q : 32 * q + 16, 0:T].bitcast(I32),
                     in_=x_scales[0:SHARED_PASSES, 4 * q : 4 * q + 4, :].bitcast(I32),
                 )
@@ -215,45 +203,45 @@ def tile_moe_two_lin_bias_kernel(tc, x_words, x_scales, w, b, gate, offs, dst, o
         def scatter_on_vector(e, gated):
             nc.vector.tensor_tensor(out_sb[:].indirect(places(e * C, VECTOR_SLOTS[e])), gated[:], bias_of(e), ADD)
 
-        nc.sync.dma_start(offs_sb[:], offs)
-        load_tokens(0)
-        nc.sync.dma_start(dst_sb[:], dst)
-        load_scales()
-
-        for a in range(1, PASSES_AHEAD_OF_MOVES):
-            tok_words.append(staged.tile([P, T], I32, name="tok_words%d" % a, offset=words_at(a)))
-        b_sb = staged.tile([P, E], F32, name="b_sb", offset=b_at)
-        gate_cols = staged.tile([P, SLOTS // P], F32, name="gate_cols", offset=gate_at)
         w_raw = [raw_tile(c) for c in range(CHUNKS_AHEAD_OF_MOVES)]
+        load_scales()
+        load_tokens(0)
+        nc.sync.dma_start(offs_sb[:], offs)
         load_tokens(1)
         load_w(0)
         nc.sync.dma_start(out=gate_cols[:], in_=gate[0, :].rearrange("(p j) -> p j", p=P))
-        nc.sync.dma_start(out=b_sb[:], in_=b)
+        nc.sync.dma_start(out=scale_rows[16:32, 0:T].bitcast(I32), in_=x_scales[PASSES - 1].bitcast(I32))
         load_tokens(2)
         load_w(1)
+        nc.sync.dma_start(out=b_sb[:], in_=b)
+        nc.sync.dma_start(dst_sb[:], dst)
         load_w(2)
+        load_tokens(3)
+        load_w(3)
+        load_tokens(4)
+        load_w(4)
 
         gather_words(0)
+        gather_words(1)
+        gather_words(2)
         nc.vector.tensor_copy(slot_scales[:], tok_scales.indirect(offs_sb[:]))
         move_last_scales()
-        for a in range(PASSES_AHEAD_OF_MOVES, PASSES):
-            tok_words.append(staged.tile([P, T], I32, name="tok_words%d" % a, offset=words_at(a)))
-            load_tokens(a)
+        slot_words[3] = staged.tile([P, SLOTS], U32, name="slot_words3", offset=held_words_at, align_bytes=DMA_ALIGN)
         for c in range(CHUNKS_AHEAD_OF_MOVES, len(CHUNKS)):
             w_raw.append(raw_tile(c))
             load_w(c)
 
-        gather_words(1)
-        spread_gate()
         round_chunk(0)
-        gather_words(2)
-        quantize_chunk(0)
+        spread_gate()
         round_chunk(1)
         gather_words(3)
+        quantize_chunk(0)
         quantize_chunk(1)
         gather_words(4)
         round_chunk(2)
+        round_chunk(3)
         quantize_chunk(2)
+        quantize_chunk(3)
         for c in range(CHUNKS_AMONG_GATHERS):
             multiply_chunk(c)
 

@@ -31,7 +31,7 @@ DMA_ALIGN = 256
 HALF = C // 2
 
 CHUNKS = [2] * 17 + [1, 2, 1, 1, 1]
-CHUNKS_AHEAD_OF_MOVES = 5
+CHUNKS_AHEAD_OF_MOVES = 7
 CHUNKS_AMONG_GATHERS = 4
 ACC_BANKS = 5
 
@@ -219,7 +219,8 @@ def tile_moe_two_lin_bias_kernel(tc, x_words, x_scales, w, b, gate, offs, dst, o
         load_tokens(3)
         load_w(3)
         load_tokens(4)
-        load_w(4)
+        for c in range(4, CHUNKS_AHEAD_OF_MOVES):
+            load_w(c)
 
         gather_words(0)
         gather_words(1)

from contextlib import ExitStack

import concourse.mybir as mybir
from concourse.masks import make_identity

K, T, E, C, N = 2560, 1536, 8, 128, 128
SLOTS = E * C
FLOPS = 2 * K * N * SLOTS

F32 = mybir.dt.float32
BF16 = mybir.dt.bfloat16
I32 = mybir.dt.int32
U32 = mybir.dt.uint32
U16 = mybir.dt.uint16
U8 = mybir.dt.uint8
FP8X4 = mybir.dt.float8_e4m3fn_x4
ADD = mybir.AluOpType.add
MULT = mybir.AluOpType.mult
COPY = mybir.ActivationFunctionType.Copy

P = 128
PACK = 4
PASSES = K // (P * PACK)
UNITS = E * PASSES
SHARED_PASSES = 4
LIST_ROWS = 16
BANK = 512
RUN = 4
DMA_ALIGN = 256

HALF = C // 2

CHUNKS = [2] * 17 + [1, 2, 1, 1, 1]
CHUNKS_AHEAD_OF_MOVES = 7
CHUNKS_AMONG_GATHERS = 4
ACC_BANKS = 5

GROUPS = [(0, 1, 2), (3, 4)]
CHUNKS_AHEAD = [2, 1]
SPLIT_EXPERT = 5
VECTOR_SLOTS = {SPLIT_EXPERT: HALF, E - 1: C}


def tile_moe_two_lin_bias_kernel(tc, x_words, x_scales, w, b, gate, offs, dst, out):
    nc = tc.nc
    with ExitStack() as ctx:
        keep = ctx.enter_context(tc.tile_pool(name="keep", bufs=1))
        staged = ctx.enter_context(tc.tile_pool(name="staged", bufs=1))
        psum = ctx.enter_context(tc.psum_pool(name="psum", bufs=1))
        psum_acc = ctx.enter_context(tc.psum_pool(name="psum_acc", bufs=ACC_BANKS))

        offs_sb = keep.tile([P, SLOTS // LIST_ROWS], U16, name="offs_sb")
        dst_sb = keep.tile([P, SLOTS // LIST_ROWS], U16, name="dst_sb")
        ident = keep.tile([P, P], F32, name="ident")
        gate_sb = keep.tile([P, SLOTS], F32, name="gate_sb")
        gated_bias = keep.tile([P, HALF + C], F32, name="gated_bias")
        out_sb = keep.tile([P, T], F32, name="out_sb", align_bytes=DMA_ALIGN)
        tok_words = [keep.tile([P, T], I32, name="tok_words%d" % a, align_bytes=DMA_ALIGN) for a in range(PASSES)]
        b_sb = keep.tile([P, E], F32, name="b_sb")
        gate_cols = keep.tile([P, SLOTS // P], F32, name="gate_cols")
        slot_words = {a: keep.tile([P, SLOTS], U32, name="slot_words%d" % a, align_bytes=64) for a in range(PASSES) if a != 3}
        slot_scales = keep.tile([P, SLOTS], U8, name="slot_scales", align_bytes=64)
        slot_scales_last = keep.tile([P, SLOTS], U8, name="slot_scales_last", align_bytes=64)
        w_bf = [keep.tile([P, u, N, PACK], BF16, name="w_bf%d" % c, align_bytes=64) for c, u in enumerate(CHUNKS)]
        w_codes = [keep.tile([P, u, N], U32, name="w_codes%d" % c, align_bytes=64) for c, u in enumerate(CHUNKS)]
        w_scales = [keep.tile([P, u, N], U8, name="w_scales%d" % c, align_bytes=64) for c, u in enumerate(CHUNKS)]
        w_rows = w.rearrange("e k n -> (e k) n")

        chunk_first = [sum(CHUNKS[:c]) for c in range(len(CHUNKS))]
        chunk_of = [c for c, u in enumerate(CHUNKS) for i in range(u)]
        last_chunk = len(CHUNKS) - 1

        def closing_chunk(e):
            return chunk_of[(e + 1) * PASSES - 1]

        vector_chunks = [closing_chunk(E - 2), last_chunk - 2, last_chunk]
        for group, ahead in zip(GROUPS, CHUNKS_AHEAD):
            first = closing_chunk(group[-1]) + ahead + 1
            vector_chunks.extend(range(first, first + len(group)))

        unit_bytes = PACK * N * 4
        later_at = chunk_first[CHUNKS_AHEAD_OF_MOVES] * unit_bytes
        held_words_at = UNITS * unit_bytes
        staged_bytes = held_words_at + SLOTS * 4

        def raw_at(c):
            return chunk_first[c] * unit_bytes

        def raw_tile(c):
            return staged.tile([P, CHUNKS[c], PACK, N], F32, name="w_raw%d" % c, offset=raw_at(c))

        scale_rows = staged.tile([P, staged_bytes - later_at], U8, name="scale_rows", offset=later_at, align_bytes=DMA_ALIGN)
        tok_scales = scale_rows[:, 0:T]

        nc.vector.memset(tok_scales.bitcast(I32), 0)
        nc.vector.memset(slot_scales_last[:].bitcast(I32), 0)
        nc.vector.memset(out_sb[:], 0.0)
        make_identity(nc, ident[:])

        def load_tokens(a):
            nc.sync.dma_start(out=tok_words[a][:], in_=x_words[a].rearrange("p t r -> p (t r)").bitcast(I32))

        def load_scales():
            for q in range(4):
                nc.gpsimd.dma_start(
                    out=scale_rows[32 * q : 32 * q + 16, 0:T].bitcast(I32),
                    in_=x_scales[0:SHARED_PASSES, 4 * q : 4 * q + 4, :].bitcast(I32),
                )

        def move_last_scales():
            for r in range(4):
                nc.sync.dma_start(
                    out=slot_scales_last[r:P:32, :].bitcast(I32),
                    in_=slot_scales[16 + r : 32 : 4, :].bitcast(I32),
                )

        def load_w(c):
            rows = w_rows[chunk_first[c] * P * PACK : (chunk_first[c] + CHUNKS[c]) * P * PACK, :]
            nc.sync.dma_start(
                out=w_raw[c][:].rearrange("p u j n -> p u (j n)"),
                in_=rows.rearrange("(u p j) n -> p u (j n)", p=P, j=PACK),
            )

        def spread_gate():
            per_bank = BANK // P
            for h in range(SLOTS // BANK):
                spread = psum.tile([P, per_bank, P], F32, name="spread%d" % h)
                for i in range(per_bank):
                    j = h * per_bank + i
                    nc.tensor.transpose(spread[:, i, :], gate_cols[:, j : j + 1].to_broadcast([P, P]), ident[:])
                nc.scalar.copy(
                    out=gate_sb[:].rearrange("n (p j) -> n p j", p=P)[:, :, h * per_bank : (h + 1) * per_bank],
                    in_=spread[:].rearrange("n j p -> n p j"),
                )
            for e in VECTOR_SLOTS:
                nc.scalar.activation(out=bias_of(e), in_=gate_sb[:, vector_slots(e)], func=COPY, scale=b_sb[:, e : e + 1])

        def slots(e):
            return slice(e * C, (e + 1) * C)

        def vector_slots(e):
            return slice(e * C, e * C + VECTOR_SLOTS[e])

        def bias_of(e):
            return gated_bias[:, 0:HALF] if e == SPLIT_EXPERT else gated_bias[:, HALF:]

        def places(first_slot, count):
            return dst_sb[:, first_slot // LIST_ROWS : (first_slot + count) // LIST_ROWS]

        def gather_words(a):
            nc.vector.tensor_copy(slot_words[a][:], tok_words[a][:].bitcast(U32).indirect(offs_sb[:]))

        def round_chunk(c):
            rounded = w_bf[c][:].rearrange("p u (g m) j -> p u g j m", m=RUN)
            raw = w_raw[c][:].rearrange("p u j (g m) -> p u g j m", m=RUN)
            if c in vector_chunks:
                nc.vector.tensor_copy(out=rounded, in_=raw)
            else:
                nc.scalar.copy(out=rounded, in_=raw)

        def quantize_chunk(c):
            nc.vector.quantize_mx(
                out=w_codes[c][:].rearrange("p u n -> p (u n)").bitcast(FP8X4),
                scales=w_scales[c][:].rearrange("p u n -> p (u n)"),
                in_=w_bf[c][:].rearrange("p u n j -> p (u n j)"),
            )

        sums = {}

        def multiply_chunk(c):
            for i in range(CHUNKS[c]):
                e, a = divmod(chunk_first[c] + i, PASSES)
                if a == 0:
                    sums[e] = psum_acc.tile([P, C], F32, name="sums")
                nc.tensor.matmul_mx(
                    out=sums[e][:],
                    lhsT=w_codes[c][:, i, :].bitcast(FP8X4),
                    lhsT_scale=w_scales[c][:, i, :],
                    rhs=slot_words[a][:, slots(e)].bitcast(FP8X4),
                    rhs_scale=slot_scales[4 * a :, slots(e)] if a < SHARED_PASSES else slot_scales_last[:, slots(e)],
                    start=(a == 0),
                    stop=(a == PASSES - 1),
                )

        def add_bias_and_gate(gated, e, first):
            nc.vector.scalar_tensor_tensor(
                out=gated,
                in0=sums[e][:, first:C],
                scalar=b_sb[:, e : e + 1],
                in1=gate_sb[:, e * C + first : (e + 1) * C],
                op0=ADD,
                op1=MULT,
            )

        def scatter_on_scalar(first_slot, count, gated):
            nc.scalar.activation(out_sb[:].indirect(places(first_slot, count)), gated[:], COPY)

        def gate_alone(e, gated):
            nc.vector.tensor_tensor(
                out=gated[:], in0=sums[e][:, 0 : VECTOR_SLOTS[e]], in1=gate_sb[:, vector_slots(e)], op=MULT
            )

        def scatter_on_vector(e, gated):
            nc.vector.tensor_tensor(out_sb[:].indirect(places(e * C, VECTOR_SLOTS[e])), gated[:], bias_of(e), ADD)

        w_raw = [raw_tile(c) for c in range(CHUNKS_AHEAD_OF_MOVES)]
        load_scales()
        load_tokens(0)
        nc.sync.dma_start(offs_sb[:], offs)
        load_tokens(1)
        load_w(0)
        nc.sync.dma_start(out=gate_cols[:], in_=gate[0, :].rearrange("(p j) -> p j", p=P))
        nc.sync.dma_start(out=scale_rows[16:32, 0:T].bitcast(I32), in_=x_scales[PASSES - 1].bitcast(I32))
        load_tokens(2)
        load_w(1)
        nc.sync.dma_start(out=b_sb[:], in_=b)
        nc.sync.dma_start(dst_sb[:], dst)
        load_w(2)
        load_tokens(3)
        load_w(3)
        load_tokens(4)
        for c in range(4, CHUNKS_AHEAD_OF_MOVES):
            load_w(c)

        gather_words(0)
        gather_words(1)
        gather_words(2)
        nc.vector.tensor_copy(slot_scales[:], tok_scales.indirect(offs_sb[:]))
        move_last_scales()
        slot_words[3] = staged.tile([P, SLOTS], U32, name="slot_words3", offset=held_words_at, align_bytes=DMA_ALIGN)
        for c in range(CHUNKS_AHEAD_OF_MOVES, len(CHUNKS)):
            w_raw.append(raw_tile(c))
            load_w(c)

        round_chunk(0)
        spread_gate()
        round_chunk(1)
        gather_words(3)
        quantize_chunk(0)
        quantize_chunk(1)
        gather_words(4)
        round_chunk(2)
        round_chunk(3)
        quantize_chunk(2)
        quantize_chunk(3)
        for c in range(CHUNKS_AMONG_GATHERS):
            multiply_chunk(c)

        gated_groups = {}
        for c in range(CHUNKS_AMONG_GATHERS, len(CHUNKS)):
            round_chunk(c)
            for group, ahead in zip(GROUPS, CHUNKS_AHEAD):
                closing = closing_chunk(group[-1])
                if c == closing + 1:
                    at = raw_at(closing + ahead - 1)
                    gated_groups[group] = staged.tile([P, len(group) * C], F32, name="gated%d" % group[0], offset=at)
                    for i, e in enumerate(group):
                        add_bias_and_gate(gated_groups[group][:, slots(i)], e, 0)
                if c == closing + 2:
                    scatter_on_scalar(group[0] * C, len(group) * C, gated_groups[group])
            if c == closing_chunk(E - 2) + 1:
                gated_rest = staged.tile([P, HALF + C], F32, name="gated_rest", offset=raw_at(c))
                add_bias_and_gate(gated_rest[:, 0:HALF], SPLIT_EXPERT, HALF)
                add_bias_and_gate(gated_rest[:, HALF:], E - 2, 0)
            behind_split_expert = c == closing_chunk(SPLIT_EXPERT) + 1
            if behind_split_expert:
                gated_half = staged.tile([P, HALF], F32, name="gated_half", offset=raw_at(c))
                gate_alone(SPLIT_EXPERT, gated_half)
            quantize_chunk(c)
            multiply_chunk(c)
            if c == last_chunk - 1:
                scatter_on_scalar(SPLIT_EXPERT * C + HALF, HALF + C, gated_rest)
            if behind_split_expert:
                scatter_on_vector(SPLIT_EXPERT, gated_half)
        gated_last = keep.tile([P, C], F32, name="gated_last")
        gate_alone(E - 1, gated_last)
        scatter_on_vector(E - 1, gated_last)

        nc.sync.dma_start(out=out, in_=out_sb[:])
